import numpy as np
import ml_dtypes


def mxq(x, axis, fmt="e4m3"):
    dtype, down = {"e4m3": (ml_dtypes.float8_e4m3fn, 7), "e5m2": (ml_dtypes.float8_e5m2, 14)}[fmt]
    v = np.moveaxis(np.asarray(x, np.float32).astype(ml_dtypes.bfloat16).astype(np.float64), axis, -1)
    blocks = v.reshape(v.shape[:-1] + (-1, 32))
    amax = np.abs(blocks).max(-1, keepdims=True)
    byte = np.maximum(np.where(amax > 0, np.frexp(amax)[1] - 1 + 127, 0) - down, 1)
    scale = np.exp2(byte - 127.0)
    codes = (blocks / scale).astype(np.float32).astype(dtype).astype(np.float64)
    return np.moveaxis((codes * scale).reshape(v.shape), -1, axis)


WIDE = False


def mx_kscale(k):
    if not WIDE:
        return np.ones(k)
    levels = np.array([10, -10, 5, -5, 0])
    if k % 512:
        return np.exp2(np.random.permutation(np.resize(levels, k // 32))).repeat(32)
    a = np.empty((k // 512, 16))
    for p in range(k // 512):
        a[p, :8] = np.random.permutation(np.resize(levels, 8))
        for g in range(8):
            far = levels[np.abs(levels - a[p, g]) >= 10]
            a[p, g + 8] = far[np.random.randint(len(far))]
    return np.exp2(a.ravel()).repeat(32)


def f64(x):
    return np.asarray(x).astype(np.float64)


def striped(idx):
    return np.tile(idx.reshape(-1, 16).T, (8, 1)).astype(np.uint16)


def unstriped(offs):
    return offs[:16].T.reshape(-1).astype(np.int64)


def pack_weight(w):
    k, n = w.shape
    w = f64(np.asarray(w, np.float32).astype(ml_dtypes.bfloat16)).reshape(k // 32, 32, n)
    amax = np.abs(w).max(1)
    byte = np.clip(np.where(amax > 0, np.frexp(amax)[1] - 1 + 127 - 7, 1), 1, 254)
    scaled = (w * np.exp2(127.0 - byte)[:, None, :]).reshape(k, n).astype(np.float32)
    words = np.ascontiguousarray(scaled.reshape(k // 512, 128, 4, n).transpose(0, 1, 3, 2)).astype(ml_dtypes.float8_e4m3fn).view(np.uint8)
    return words, np.ascontiguousarray(byte.astype(np.uint8).reshape(k // 512, 16, n))


def unpack_weight(words, scales):
    g, p, n, _ = words.shape
    vals = np.ascontiguousarray(words).view(ml_dtypes.float8_e4m3fn).astype(np.float64) * np.repeat(np.exp2(scales.astype(np.float64) - 127.0), 8, axis=1)[..., None]
    return vals.transpose(0, 1, 3, 2).reshape(g * 512, n)


def relu(v):
    return np.maximum(v, 0.0)


def sigmoid(v):
    return 1.0 / (1.0 + np.exp(-np.maximum(v, -700.0)))


K, T, S, V, H, W, G = 512, 2048, 512, 512, 512, 1024, 1024


def setup_inputs():
    n = np.random.standard_normal
    s = mx_kscale(K)[:, None]
    u = mx_kscale(H)
    packed_xT = pack_weight(n((K, T)) * s)
    packed_eT = pack_weight(n((K, W)) / np.sqrt(2 * K) / s)
    packed_vT = pack_weight(n((H, G)) / np.sqrt(2 * H) / u[:, None])
    return {
        "x_words": packed_xT[0],
        "x_scales": packed_xT[1],
        "e_words": packed_eT[0],
        "e_scales": packed_eT[1],
        "v_words": packed_vT[0],
        "v_scales": packed_vT[1],
        "gT": (n((K, S)) * s).astype(np.float32),
        "w1": (n((K, H)) / np.sqrt(K) / s * u).astype(np.float32),
        "offs": striped(np.random.permutation(T)[:S]),
        "cand": striped(np.random.permutation(W)[:V]),
    }


def reference(x_words, x_scales, e_words, e_scales, v_words, v_scales, gT, w1, offs, cand):
    xq = unpack_weight(x_words, x_scales)[:, unstriped(offs)]
    e_cand = unpack_weight(e_words, e_scales)[:, unstriped(cand)]
    gTq = mxq(f64(gT), 0, "e4m3")
    h = relu(mxq(f64(w1), 0, "e4m3").T @ gTq)
    v_cand = unpack_weight(v_words, v_scales)[:, unstriped(cand)]
    y = xq.T @ e_cand + mxq(h, 0, "e4m3").T @ v_cand
    return sigmoid(y)

@@ -1,0 +1,140 @@
+from contextlib import ExitStack
+
+import concourse.mybir as mybir
+
+F32 = mybir.dt.float32
+BF16 = mybir.dt.bfloat16
+I32 = mybir.dt.int32
+U32 = mybir.dt.uint32
+U16 = mybir.dt.uint16
+U8 = mybir.dt.uint8
+FP8X4 = mybir.dt.float8_e4m3fn_x4
+ACT = mybir.ActivationFunctionType
+
+P = 128
+PACK = 4
+K, T, S, V, H, W = 512, 2048, 512, 512, 512, 1024
+FLOPS = 2 * K * H * S + 2 * K * S * V + 2 * H * S * V
+X_ROW, E_ROW, V_ROW = 0, 4, 8
+
+
+def tile_picked_zwd_sigmoid_p_kernel(tc, x_words, x_scales, e_words, e_scales, v_words, v_scales, gT, w1, offs, cand, out):
+    nc = tc.nc
+    with ExitStack() as ctx:
+        lists = ctx.enter_context(tc.tile_pool(name="lists", bufs=1))
+        sb = ctx.enter_context(tc.tile_pool(name="sb", bufs=1))
+        psum = ctx.enter_context(tc.psum_pool(name="psum", bufs=1))
+
+        offs_sb = lists.tile([P, S // 16], U16, name="offs_sb")
+        cand_sb = lists.tile([P, V // 16], U16, name="cand_sb")
+
+        def tile(shape, dtype, name, tag=None):
+            return sb.tile(shape, dtype, name=name, tag=tag or name, align_bytes=64)
+
+        def load_words(words, name):
+            t = tile([P, words.shape[2]], I32, name)
+            nc.sync.dma_start(out=t[:], in_=words[0].rearrange("p n t -> p (n t)").bitcast(I32))
+            return t
+
+        def load_scales(queue, t, scales, row):
+            rows = scales[0].rearrange("(q r) n -> r q n", r=4)
+            for r in range(4):
+                queue.dma_start(out=t[row + r : P : 32, :].bitcast(I32), in_=rows[r].bitcast(I32))
+
+        def load_half(src, half, name):
+            t = tile([P, PACK, 256], F32, name)
+            nc.sync.dma_start(out=t[:], in_=src.rearrange("(p j) c -> p j c", j=PACK)[:, :, 256 * half : 256 * (half + 1)])
+            return t
+
+        def gather(window, dtype, offsets, n, name, tag=None):
+            t = tile([P, n], dtype, name, tag)
+            nc.vector.tensor_copy(out=t[:], in_=window[:].bitcast(dtype).indirect(offsets))
+            return t
+
+        def quantize(src, n, name, tag=None, ptag=None):
+            codes = tile([P, n], U32, name + "_codes", tag)
+            plane = tile([P, n], U8, name + "_plane", ptag)
+            nc.vector.quantize_mx(out=codes[:].bitcast(FP8X4), scales=plane[:], in_=src)
+            return codes, plane
+
+        es_tab = tile([P, W], U8, "es_tab")
+        xs_tab = tile([P, T], U8, "xs_tab")
+        vs_tab = tile([P, W], U8, "vs_tab")
+        for t in (es_tab, vs_tab, xs_tab):
+            nc.vector.memset(t[:].bitcast(I32), 0)
+
+        warm_in = tile([P, 1], F32, "warm_in")
+        warm_out = tile([P, 1], F32, "warm_out")
+        nc.gpsimd.memset(warm_in[:], 0.0)
+        nc.scalar.activation(warm_out[:], warm_in[:], ACT.Sigmoid)
+
+        nc.sync.dma_start(cand_sb[:], cand)
+        e_tab = load_words(e_words, "e_tab")
+        load_scales(nc.sync, es_tab, e_scales, E_ROW)
+        w_raw = [load_half(w1, 0, "w_raw0")]
+        w_raw.append(load_half(w1, 1, "w_raw1"))
+        load_scales(nc.sync, vs_tab, v_scales, V_ROW)
+        g_raw = [load_half(gT, 0, "g_raw0")]
+        nc.sync.dma_start(offs_sb[:], offs)
+        g_raw.append(load_half(gT, 1, "g_raw1"))
+        load_scales(nc.sync, xs_tab, x_scales, X_ROW)
+        v_tab = load_words(v_words, "v_tab")
+        x_tab = load_words(x_words, "x_tab")
+
+        e_plane = gather(es_tab, U8, cand_sb[:], V, "e_plane")
+        x_plane = gather(xs_tab, U8, offs_sb[:], S, "x_plane", None)
+
+        w_bf = tile([P, H * PACK], BF16, "w_bf")
+        w_view = w_bf[:].rearrange("p (t m j) -> p m j t", t=PACK, j=PACK)
+        for half in range(2):
+            nc.scalar.copy(out=w_view[:, 64 * half : 64 * (half + 1)], in_=w_raw[half][:].rearrange("p j (m t) -> p m j t", t=PACK))
+        v_plane = gather(vs_tab, U8, cand_sb[:], V, "v_plane")
+        w_codes, w_plane = quantize(w_bf[:], H, "w", "vs_tab")
+
+        g_q = []
+        for half in range(2):
+            g_bf = tile([P, 256 * PACK], BF16, f"g_bf{half}")
+            nc.scalar.copy(
+                out=g_bf[:].rearrange("p (c i j) -> p c j i", i=4, j=PACK),
+                in_=g_raw[half][:].rearrange("p j (c i) -> p c j i", i=4),
+            )
+            g_q.append(quantize(g_bf[:], 256, f"g{half}", (None, "xs_tab")[half]))
+        v_codes = gather(v_tab, U32, cand_sb[:], V, "v_codes", "g_bf1")
+        e_codes = gather(e_tab, U32, cand_sb[:], V, "e_codes", None)
+
+        hq = []
+        hb = []
+        for c in range(4):
+            g_codes, g_plane = g_q[c // 2]
+            cols = slice(P * (c % 2), P * (c % 2 + 1))
+            h_ps = psum.tile([P, PACK, P], F32, name=f"h_ps{c}")
+            for t in range(PACK):
+                ch = slice(P * t, P * (t + 1))
+                nc.tensor.matmul_mx(out=h_ps[:, t, :], lhsT=w_codes[:, ch].bitcast(FP8X4), lhsT_scale=w_plane[:, ch],
+                                    rhs=g_codes[:, cols].bitcast(FP8X4), rhs_scale=g_plane[:, cols], start=True, stop=True)
+            if c == 2:
+                x_codes = tile([P, S], U32, "x_codes", "h_bf0")
+                for half in range(2):
+                    nc.vector.tensor_copy(out=x_codes[:, 256 * half : 256 * (half + 1)], in_=x_tab[:].bitcast(U32).indirect(offs_sb[:, 16 * half : 16 * (half + 1)]))
+            if c % 2 == 0:
+                h_bf2 = tile([P, 2, P * PACK], BF16, f"h_bf{c // 2}", ("g_raw1", None)[c // 2])
+                h_codes2 = tile([P, 2 * P], U32, f"h_codes{c // 2}", ("v_tab", "x_tab")[c // 2])
+                h_plane2 = tile([P, 2 * P], U8, f"h_plane{c // 2}", (None, None)[c // 2])
+            h_bf = h_bf2[:, c % 2, :]
+            nc.scalar.activation(h_bf.rearrange("p (n t) -> p n t", t=PACK), h_ps[:].rearrange("p t n -> p n t"), ACT.Relu)
+            hb.append(h_bf)
+            h_codes, h_plane = h_codes2[:, cols], h_plane2[:, cols]
+            nc.vector.quantize_mx(out=h_codes.bitcast(FP8X4), scales=h_plane, in_=h_bf)
+            hq.append((h_codes, h_plane))
+
+        for c in range(4):
+            cols = slice(P * (c % 2), P * (c % 2 + 1))
+            deep = (hq[c][0], hq[c][1], v_codes[:], v_plane[V_ROW:P, :])
+            wide = (x_codes[:, P * c : P * (c + 1)], x_plane[:, P * c : P * (c + 1)], e_codes[:], e_plane[E_ROW:P, :])
+            y_ps = psum.tile([P, V], F32, name=f"y_ps{c}")
+            for k, (lc, lp, rc, rp) in enumerate((deep, wide) if c < 2 else (wide, deep)):
+                nc.tensor.matmul_mx(out=y_ps[:], lhsT=lc.bitcast(FP8X4), lhsT_scale=lp, rhs=rc.bitcast(FP8X4), rhs_scale=rp, start=(k == 0), stop=(k == 1))
+            for n0, n1 in (((0, 256), (256, 512)) if c == 3 else ((0, V),)):
+                res = tile([P, n1 - n0], F32, f"res{c}_{n0}")
+                nc.scalar.activation(res[:], y_ps[:, n0:n1], ACT.Sigmoid)
+                (nc.scalar if n1 == V and c == 3 else nc.sync).dma_start(out=out[P * c : P * (c + 1), n0:n1], in_=res[:])

@@ -13,9 +13,14 @@ ACT = mybir.ActivationFunctionType
 
 P = 128
 PACK = 4
-K, T, S, V, H, W = 512, 2048, 512, 512, 512, 1024
+QUAD = 32
+LIST_ROWS = 16
+K, H = 512, 512
+T, W = 2048, 1024
+S, V = 512, 512
+HALF = 256
+V_ROW = 8
 FLOPS = 2 * K * H * S + 2 * K * S * V + 2 * H * S * V
-X_ROW, E_ROW, V_ROW = 0, 4, 8
 
 
 def tile_picked_zwd_sigmoid_p_kernel(tc, x_words, x_scales, e_words, e_scales, v_words, v_scales, gT, w1, offs, cand, out):
@@ -25,116 +30,137 @@ def tile_picked_zwd_sigmoid_p_kernel(tc, x_words, x_scales, e_words, e_scales, v
         sb = ctx.enter_context(tc.tile_pool(name="sb", bufs=1))
         psum = ctx.enter_context(tc.psum_pool(name="psum", bufs=1))
 
-        offs_sb = lists.tile([P, S // 16], U16, name="offs_sb")
-        cand_sb = lists.tile([P, V // 16], U16, name="cand_sb")
+        offs_sb = lists.tile([P, S // LIST_ROWS], U16, name="offs_sb")
+        cand_sb = lists.tile([P, V // LIST_ROWS], U16, name="cand_sb")
 
-        def tile(shape, dtype, name, tag=None):
-            return sb.tile(shape, dtype, name=name, tag=tag or name, align_bytes=64)
+        def tile(shape, dtype, name, reuse=None):
+            return sb.tile(shape, dtype, name=name, tag=reuse or name, align_bytes=64)
 
         def load_words(words, name):
-            t = tile([P, words.shape[2]], I32, name)
-            nc.sync.dma_start(out=t[:], in_=words[0].rearrange("p n t -> p (n t)").bitcast(I32))
-            return t
+            table = tile([P, words.shape[2]], I32, name)
+            nc.sync.dma_start(out=table[:], in_=words[0].rearrange("p n t -> p (n t)").bitcast(I32))
+            return table
 
-        def load_scales(queue, t, scales, row):
-            rows = scales[0].rearrange("(q r) n -> r q n", r=4)
-            for r in range(4):
-                queue.dma_start(out=t[row + r : P : 32, :].bitcast(I32), in_=rows[r].bitcast(I32))
+        def load_v_scales(queue, rows_in_quadrant):
+            rows = v_scales[0].rearrange("(q r) n -> r q n", r=4)
+            for r in rows_in_quadrant:
+                queue.dma_start(out=vs_tab[V_ROW + r : P : QUAD, :].bitcast(I32), in_=rows[r].bitcast(I32))
 
         def load_half(src, half, name):
-            t = tile([P, PACK, 256], F32, name)
-            nc.sync.dma_start(out=t[:], in_=src.rearrange("(p j) c -> p j c", j=PACK)[:, :, 256 * half : 256 * (half + 1)])
-            return t
+            raw = tile([P, PACK, HALF], F32, name)
+            nc.sync.dma_start(out=raw[:], in_=src.rearrange("(p j) c -> p j c", j=PACK)[:, :, HALF * half : HALF * (half + 1)])
+            return raw
 
-        def gather(window, dtype, offsets, n, name, tag=None):
-            t = tile([P, n], dtype, name, tag)
-            nc.vector.tensor_copy(out=t[:], in_=window[:].bitcast(dtype).indirect(offsets))
-            return t
+        def gather(window, dtype, offsets, n, name, reuse=None):
+            picked = tile([P, n], dtype, name, reuse)
+            nc.vector.tensor_copy(out=picked[:], in_=window[:].bitcast(dtype).indirect(offsets))
+            return picked
 
-        def quantize(src, n, name, tag=None, ptag=None):
-            codes = tile([P, n], U32, name + "_codes", tag)
-            plane = tile([P, n], U8, name + "_plane", ptag)
+        def quantize(src, n, name):
+            codes = tile([P, n], U32, name + "_codes")
+            plane = tile([P, n], U8, name + "_plane")
             nc.vector.quantize_mx(out=codes[:].bitcast(FP8X4), scales=plane[:], in_=src)
             return codes, plane
 
         es_tab = tile([P, W], U8, "es_tab")
         xs_tab = tile([P, T], U8, "xs_tab")
         vs_tab = tile([P, W], U8, "vs_tab")
-        for t in (es_tab, vs_tab, xs_tab):
-            nc.vector.memset(t[:].bitcast(I32), 0)
+        ex_plane = tile([P, V + S], U8, "ex_plane")
+        for cleared in (es_tab, xs_tab, ex_plane):
+            nc.vector.memset(cleared[:].bitcast(I32), 0)
 
         warm_in = tile([P, 1], F32, "warm_in")
         warm_out = tile([P, 1], F32, "warm_out")
         nc.gpsimd.memset(warm_in[:], 0.0)
+        nc.gpsimd.memset(vs_tab[:].bitcast(I32), 0)
         nc.scalar.activation(warm_out[:], warm_in[:], ACT.Sigmoid)
 
-        nc.sync.dma_start(cand_sb[:], cand)
-        e_tab = load_words(e_words, "e_tab")
-        load_scales(nc.sync, es_tab, e_scales, E_ROW)
         w_raw = [load_half(w1, 0, "w_raw0")]
-        w_raw.append(load_half(w1, 1, "w_raw1"))
-        load_scales(nc.sync, vs_tab, v_scales, V_ROW)
-        g_raw = [load_half(gT, 0, "g_raw0")]
+        nc.sync.dma_start(cand_sb[:], cand)
+        nc.sync.dma_start(out=es_tab[0:P:8, :].bitcast(I32), in_=e_scales[0].bitcast(I32))
+        load_v_scales(nc.gpsimd, (0, 1))
         nc.sync.dma_start(offs_sb[:], offs)
+        nc.sync.dma_start(out=xs_tab[0:P:8, :].bitcast(I32), in_=x_scales[0].bitcast(I32))
+        w_raw.append(load_half(w1, 1, "w_raw1"))
+        e_tab = load_words(e_words, "e_tab")
+        load_v_scales(nc.sync, (2, 3))
+        g_raw = [load_half(gT, 0, "g_raw0")]
         g_raw.append(load_half(gT, 1, "g_raw1"))
-        load_scales(nc.sync, xs_tab, x_scales, X_ROW)
         v_tab = load_words(v_words, "v_tab")
         x_tab = load_words(x_words, "x_tab")
 
-        e_plane = gather(es_tab, U8, cand_sb[:], V, "e_plane")
-        x_plane = gather(xs_tab, U8, offs_sb[:], S, "x_plane", None)
+        ex_picked = tile([P, V + S], U8, "ex_picked")
+        nc.vector.tensor_copy(out=ex_picked[:, 0:V], in_=es_tab[:].indirect(cand_sb[:]))
+        nc.vector.tensor_copy(out=ex_picked[:, V : V + S], in_=xs_tab[:].indirect(offs_sb[:]))
+        for r in range(4):
+            nc.sync.dma_start(out=ex_plane[r:P:QUAD, :].bitcast(I32), in_=ex_picked[8 * r : P : QUAD, :].bitcast(I32))
 
         w_bf = tile([P, H * PACK], BF16, "w_bf")
         w_view = w_bf[:].rearrange("p (t m j) -> p m j t", t=PACK, j=PACK)
+        m_half = HALF // PACK
         for half in range(2):
-            nc.scalar.copy(out=w_view[:, 64 * half : 64 * (half + 1)], in_=w_raw[half][:].rearrange("p j (m t) -> p m j t", t=PACK))
-        v_plane = gather(vs_tab, U8, cand_sb[:], V, "v_plane")
-        w_codes, w_plane = quantize(w_bf[:], H, "w", "vs_tab")
+            nc.scalar.copy(out=w_view[:, m_half * half : m_half * (half + 1)], in_=w_raw[half][:].rearrange("p j (m t) -> p m j t", t=PACK))
+        w_codes, w_plane = quantize(w_bf[:], H, "w")
+
+        e_codes = gather(e_tab, U32, cand_sb[:], V, "e_codes")
 
         g_q = []
         for half in range(2):
-            g_bf = tile([P, 256 * PACK], BF16, f"g_bf{half}")
+            g_bf = tile([P, HALF * PACK], BF16, f"g_bf{half}")
             nc.scalar.copy(
                 out=g_bf[:].rearrange("p (c i j) -> p c j i", i=4, j=PACK),
                 in_=g_raw[half][:].rearrange("p j (c i) -> p c j i", i=4),
             )
-            g_q.append(quantize(g_bf[:], 256, f"g{half}", (None, "xs_tab")[half]))
-        v_codes = gather(v_tab, U32, cand_sb[:], V, "v_codes", "g_bf1")
-        e_codes = gather(e_tab, U32, cand_sb[:], V, "e_codes", None)
+            g_q.append(quantize(g_bf[:], HALF, f"g{half}"))
+            if half == 0:
+                v_plane = gather(vs_tab, U8, cand_sb[:], V, "v_plane", "g_raw0")
+        v_codes = gather(v_tab, U32, cand_sb[:], V, "v_codes", "g_raw1")
 
-        hq = []
-        hb = []
-        for c in range(4):
+        h_q = []
+        for c in range(S // P):
             g_codes, g_plane = g_q[c // 2]
             cols = slice(P * (c % 2), P * (c % 2 + 1))
-            h_ps = psum.tile([P, PACK, P], F32, name=f"h_ps{c}")
+            h_ps = psum.tile([P, PACK, P], F32, name=f"h_ps{c}", tag=f"h_ps{c}")
             for t in range(PACK):
-                ch = slice(P * t, P * (t + 1))
-                nc.tensor.matmul_mx(out=h_ps[:, t, :], lhsT=w_codes[:, ch].bitcast(FP8X4), lhsT_scale=w_plane[:, ch],
-                                    rhs=g_codes[:, cols].bitcast(FP8X4), rhs_scale=g_plane[:, cols], start=True, stop=True)
+                channels = slice(P * t, P * (t + 1))
+                nc.tensor.matmul_mx(
+                    out=h_ps[:, t, :],
+                    lhsT=w_codes[:, channels].bitcast(FP8X4),
+                    lhsT_scale=w_plane[:, channels],
+                    rhs=g_codes[:, cols].bitcast(FP8X4),
+                    rhs_scale=g_plane[:, cols],
+                    start=True,
+                    stop=True,
+                )
             if c == 2:
-                x_codes = tile([P, S], U32, "x_codes", "h_bf0")
+                x_codes = tile([P, S], U32, "x_codes")
                 for half in range(2):
-                    nc.vector.tensor_copy(out=x_codes[:, 256 * half : 256 * (half + 1)], in_=x_tab[:].bitcast(U32).indirect(offs_sb[:, 16 * half : 16 * (half + 1)]))
+                    entries = slice(HALF // LIST_ROWS * half, HALF // LIST_ROWS * (half + 1))
+                    nc.vector.tensor_copy(out=x_codes[:, HALF * half : HALF * (half + 1)], in_=x_tab[:].bitcast(U32).indirect(offs_sb[:, entries]))
             if c % 2 == 0:
-                h_bf2 = tile([P, 2, P * PACK], BF16, f"h_bf{c // 2}", ("g_raw1", None)[c // 2])
-                h_codes2 = tile([P, 2 * P], U32, f"h_codes{c // 2}", ("v_tab", "x_tab")[c // 2])
-                h_plane2 = tile([P, 2 * P], U8, f"h_plane{c // 2}", (None, None)[c // 2])
-            h_bf = h_bf2[:, c % 2, :]
-            nc.scalar.activation(h_bf.rearrange("p (n t) -> p n t", t=PACK), h_ps[:].rearrange("p t n -> p n t"), ACT.Relu)
-            hb.append(h_bf)
-            h_codes, h_plane = h_codes2[:, cols], h_plane2[:, cols]
-            nc.vector.quantize_mx(out=h_codes.bitcast(FP8X4), scales=h_plane, in_=h_bf)
-            hq.append((h_codes, h_plane))
+                h_bf = tile([P, 2, P * PACK], BF16, f"h_bf{c // 2}")
+                h_codes = tile([P, HALF], U32, f"h_codes{c // 2}", "x_tab" if c == 2 else None)
+                h_plane = tile([P, HALF], U8, f"h_plane{c // 2}")
+            nc.scalar.activation(h_bf[:, c % 2, :].rearrange("p (n t) -> p n t", t=PACK), h_ps[:].rearrange("p t n -> p n t"), ACT.Relu)
+            nc.vector.quantize_mx(out=h_codes[:, cols].bitcast(FP8X4), scales=h_plane[:, cols], in_=h_bf[:, c % 2, :])
+            h_q.append((h_codes[:, cols], h_plane[:, cols]))
 
-        for c in range(4):
-            cols = slice(P * (c % 2), P * (c % 2 + 1))
-            deep = (hq[c][0], hq[c][1], v_codes[:], v_plane[V_ROW:P, :])
-            wide = (x_codes[:, P * c : P * (c + 1)], x_plane[:, P * c : P * (c + 1)], e_codes[:], e_plane[E_ROW:P, :])
-            y_ps = psum.tile([P, V], F32, name=f"y_ps{c}")
-            for k, (lc, lp, rc, rp) in enumerate((deep, wide) if c < 2 else (wide, deep)):
-                nc.tensor.matmul_mx(out=y_ps[:], lhsT=lc.bitcast(FP8X4), lhsT_scale=lp, rhs=rc.bitcast(FP8X4), rhs_scale=rp, start=(k == 0), stop=(k == 1))
-            for n0, n1 in (((0, 256), (256, 512)) if c == 3 else ((0, V),)):
-                res = tile([P, n1 - n0], F32, f"res{c}_{n0}")
-                nc.scalar.activation(res[:], y_ps[:, n0:n1], ACT.Sigmoid)
-                (nc.scalar if n1 == V and c == 3 else nc.sync).dma_start(out=out[P * c : P * (c + 1), n0:n1], in_=res[:])
+        for c in range(S // P):
+            users = slice(P * c, P * (c + 1))
+            for n0, n1 in ((0, V // 2), (V // 2, V)) if c == 0 else ((0, V),):
+                deep = (h_q[c][0], h_q[c][1], v_codes[:, n0:n1], v_plane[V_ROW:P, n0:n1])
+                wide = (x_codes[:, users], ex_plane[:, V + P * c : V + P * (c + 1)], e_codes[:, n0:n1], ex_plane[:, n0:n1])
+                y_ps = psum.tile([P, n1 - n0], F32, name=f"y_ps{c}_{n0}", tag="h_ps0" if n0 > 0 else f"y_ps{c}")
+                for step, (user_codes, user_plane, item_codes, item_plane) in enumerate((deep, wide) if c < 2 else (wide, deep)):
+                    nc.tensor.matmul_mx(
+                        out=y_ps[:],
+                        lhsT=user_codes.bitcast(FP8X4),
+                        lhsT_scale=user_plane,
+                        rhs=item_codes.bitcast(FP8X4),
+                        rhs_scale=item_plane,
+                        start=(step == 0),
+                        stop=(step == 1),
+                    )
+                scores = tile([P, n1 - n0], F32, f"scores{c}_{n0}")
+                nc.scalar.activation(scores[:], y_ps[:], ACT.Sigmoid)
+                nc.sync.dma_start(out=out[users, n0:n1], in_=scores[:])

@@ -19,7 +19,7 @@ K, H = 512, 512
 T, W = 2048, 1024
 S, V = 512, 512
 HALF = 256
-V_ROW = 8
+W_FIRST = 2
 FLOPS = 2 * K * H * S + 2 * K * S * V + 2 * H * S * V
 
 
@@ -41,15 +41,8 @@ def tile_picked_zwd_sigmoid_p_kernel(tc, x_words, x_scales, e_words, e_scales, v
             nc.sync.dma_start(out=table[:], in_=words[0].rearrange("p n t -> p (n t)").bitcast(I32))
             return table
 
-        def load_v_scales(queue, rows_in_quadrant):
-            rows = v_scales[0].rearrange("(q r) n -> r q n", r=4)
-            for r in rows_in_quadrant:
-                queue.dma_start(out=vs_tab[V_ROW + r : P : QUAD, :].bitcast(I32), in_=rows[r].bitcast(I32))
-
-        def load_half(src, half, name):
-            raw = tile([P, PACK, HALF], F32, name)
-            nc.sync.dma_start(out=raw[:], in_=src.rearrange("(p j) c -> p j c", j=PACK)[:, :, HALF * half : HALF * (half + 1)])
-            return raw
+        def load_scales(table, rows):
+            nc.sync.dma_start(out=table[0:P:8, :].bitcast(I32), in_=rows[0].bitcast(I32))
 
         def gather(window, dtype, offsets, n, name, reuse=None):
             picked = tile([P, n], dtype, name, reuse)
@@ -63,104 +56,104 @@ def tile_picked_zwd_sigmoid_p_kernel(tc, x_words, x_scales, e_words, e_scales, v
             return codes, plane
 
         es_tab = tile([P, W], U8, "es_tab")
-        xs_tab = tile([P, T], U8, "xs_tab")
         vs_tab = tile([P, W], U8, "vs_tab")
-        ex_plane = tile([P, V + S], U8, "ex_plane")
-        for cleared in (es_tab, xs_tab, ex_plane):
+        xs_tab = tile([P, T], U8, "xs_tab")
+        planes = tile([P, 2 * V + S], U8, "planes")
+        for cleared in (es_tab, vs_tab, xs_tab, planes):
             nc.vector.memset(cleared[:].bitcast(I32), 0)
 
         warm_in = tile([P, 1], F32, "warm_in")
         warm_out = tile([P, 1], F32, "warm_out")
         nc.gpsimd.memset(warm_in[:], 0.0)
-        nc.gpsimd.memset(vs_tab[:].bitcast(I32), 0)
         nc.scalar.activation(warm_out[:], warm_in[:], ACT.Sigmoid)
 
-        w_raw = [load_half(w1, 0, "w_raw0")]
+        w_raw = tile([P, PACK, H], F32, "w_raw")
+        w_rows = w1.rearrange("(p j) c -> p j c", j=PACK)
+        nc.sync.dma_start(out=w_raw[:, 0:W_FIRST, :], in_=w_rows[:, 0:W_FIRST, :])
         nc.sync.dma_start(cand_sb[:], cand)
-        nc.sync.dma_start(out=es_tab[0:P:8, :].bitcast(I32), in_=e_scales[0].bitcast(I32))
-        load_v_scales(nc.gpsimd, (0, 1))
         nc.sync.dma_start(offs_sb[:], offs)
-        nc.sync.dma_start(out=xs_tab[0:P:8, :].bitcast(I32), in_=x_scales[0].bitcast(I32))
-        w_raw.append(load_half(w1, 1, "w_raw1"))
+        load_scales(es_tab, e_scales)
+        load_scales(vs_tab, v_scales)
+        nc.sync.dma_start(out=w_raw[:, W_FIRST:PACK, :], in_=w_rows[:, W_FIRST:PACK, :])
+        load_scales(xs_tab, x_scales)
+        g_raw = tile([P, PACK, S], F32, "g_raw")
+        nc.sync.dma_start(out=g_raw[:], in_=gT.rearrange("(p j) c -> p j c", j=PACK))
         e_tab = load_words(e_words, "e_tab")
-        load_v_scales(nc.sync, (2, 3))
-        g_raw = [load_half(gT, 0, "g_raw0")]
-        g_raw.append(load_half(gT, 1, "g_raw1"))
         v_tab = load_words(v_words, "v_tab")
-        x_tab = load_words(x_words, "x_tab")
+        x_tab = tile([P, T], I32, "x_tab")
+        x_rows = x_words[0].rearrange("p n t -> p (n t)").bitcast(I32)
+        nc.sync.dma_start(out=x_tab[:, 0 : T // 2], in_=x_rows[:, 0 : T // 2])
 
-        ex_picked = tile([P, V + S], U8, "ex_picked")
-        nc.vector.tensor_copy(out=ex_picked[:, 0:V], in_=es_tab[:].indirect(cand_sb[:]))
-        nc.vector.tensor_copy(out=ex_picked[:, V : V + S], in_=xs_tab[:].indirect(offs_sb[:]))
+        picked = tile([P, 2 * V + S], U8, "picked")
+        nc.vector.tensor_copy(out=picked[:, 0:V], in_=es_tab[:].indirect(cand_sb[:]))
+        nc.vector.tensor_copy(out=picked[:, V : 2 * V], in_=vs_tab[:].indirect(cand_sb[:]))
+        nc.vector.tensor_copy(out=picked[:, 2 * V : 2 * V + S], in_=xs_tab[:].indirect(offs_sb[:]))
         for r in range(4):
-            nc.sync.dma_start(out=ex_plane[r:P:QUAD, :].bitcast(I32), in_=ex_picked[8 * r : P : QUAD, :].bitcast(I32))
+            nc.sync.dma_start(out=planes[r:P:QUAD, :].bitcast(I32), in_=picked[8 * r : P : QUAD, :].bitcast(I32))
+        nc.sync.dma_start(out=x_tab[:, T // 2 : T], in_=x_rows[:, T // 2 : T])
 
         w_bf = tile([P, H * PACK], BF16, "w_bf")
-        w_view = w_bf[:].rearrange("p (t m j) -> p m j t", t=PACK, j=PACK)
-        m_half = HALF // PACK
-        for half in range(2):
-            nc.scalar.copy(out=w_view[:, m_half * half : m_half * (half + 1)], in_=w_raw[half][:].rearrange("p j (m t) -> p m j t", t=PACK))
+        nc.scalar.copy(out=w_bf[:].rearrange("p (t m j) -> p m j t", t=PACK, j=PACK), in_=w_raw[:].rearrange("p j (m t) -> p m j t", t=PACK))
         w_codes, w_plane = quantize(w_bf[:], H, "w")
 
-        e_codes = gather(e_tab, U32, cand_sb[:], V, "e_codes")
-
-        g_q = []
-        for half in range(2):
-            g_bf = tile([P, HALF * PACK], BF16, f"g_bf{half}")
+        g_bf = tile([P, S * PACK], BF16, "g_bf")
+        g_codes = tile([P, S], U32, "g_codes")
+        g_plane = tile([P, S], U8, "g_plane")
+        for c in range(S // P):
             nc.scalar.copy(
-                out=g_bf[:].rearrange("p (c i j) -> p c j i", i=4, j=PACK),
-                in_=g_raw[half][:].rearrange("p j (c i) -> p c j i", i=4),
+                out=g_bf[:, PACK * P * c : PACK * P * (c + 1)].rearrange("p (c i j) -> p c j i", i=4, j=PACK),
+                in_=g_raw[:, :, P * c : P * (c + 1)].rearrange("p j (c i) -> p c j i", i=4),
             )
-            g_q.append(quantize(g_bf[:], HALF, f"g{half}"))
-            if half == 0:
-                v_plane = gather(vs_tab, U8, cand_sb[:], V, "v_plane", "g_raw0")
-        v_codes = gather(v_tab, U32, cand_sb[:], V, "v_codes", "g_raw1")
+        for u0, u1 in ((0, P), (P, HALF), (HALF, S)):
+            nc.vector.quantize_mx(out=g_codes[:, u0:u1].bitcast(FP8X4), scales=g_plane[:, u0:u1], in_=g_bf[:, PACK * u0 : PACK * u1])
+        e_codes = gather(e_tab, U32, cand_sb[:], V, "e_codes")
+        v_codes = gather(v_tab, U32, cand_sb[:], V, "v_codes")
+
+        def mx_pass(acc, stationary, moving, start, stop):
+            nc.tensor.matmul_mx(
+                out=acc,
+                lhsT=stationary[0].bitcast(FP8X4),
+                lhsT_scale=stationary[1],
+                rhs=moving[0].bitcast(FP8X4),
+                rhs_scale=moving[1],
+                start=start,
+                stop=stop,
+            )
 
         h_q = []
-        for c in range(S // P):
-            g_codes, g_plane = g_q[c // 2]
-            cols = slice(P * (c % 2), P * (c % 2 + 1))
-            h_ps = psum.tile([P, PACK, P], F32, name=f"h_ps{c}", tag=f"h_ps{c}")
-            for t in range(PACK):
-                channels = slice(P * t, P * (t + 1))
-                nc.tensor.matmul_mx(
-                    out=h_ps[:, t, :],
-                    lhsT=w_codes[:, channels].bitcast(FP8X4),
-                    lhsT_scale=w_plane[:, channels],
-                    rhs=g_codes[:, cols].bitcast(FP8X4),
-                    rhs_scale=g_plane[:, cols],
-                    start=True,
-                    stop=True,
-                )
-            if c == 2:
+        for half in range(2):
+            h_bf = tile([P, 2, P * PACK], BF16, f"h_bf{half}")
+            for c in (2 * half, 2 * half + 1):
+                users = slice(P * c, P * (c + 1))
+                h_ps = psum.tile([P, PACK, P], F32, name=f"h_ps{c}", tag=f"h_ps{c}")
+                for t in range(PACK):
+                    channels = slice(P * t, P * (t + 1))
+                    mx_pass(h_ps[:, t, :], (w_codes[:, channels], w_plane[:, channels]), (g_codes[:, users], g_plane[:, users]), True, True)
+                nc.scalar.activation(h_bf[:, c % 2, :].rearrange("p (n t) -> p n t", t=PACK), h_ps[:].rearrange("p t n -> p n t"), ACT.Relu)
+            if half == 1:
                 x_codes = tile([P, S], U32, "x_codes")
-                for half in range(2):
-                    entries = slice(HALF // LIST_ROWS * half, HALF // LIST_ROWS * (half + 1))
-                    nc.vector.tensor_copy(out=x_codes[:, HALF * half : HALF * (half + 1)], in_=x_tab[:].bitcast(U32).indirect(offs_sb[:, entries]))
-            if c % 2 == 0:
-                h_bf = tile([P, 2, P * PACK], BF16, f"h_bf{c // 2}")
-                h_codes = tile([P, HALF], U32, f"h_codes{c // 2}", "x_tab" if c == 2 else None)
-                h_plane = tile([P, HALF], U8, f"h_plane{c // 2}")
-            nc.scalar.activation(h_bf[:, c % 2, :].rearrange("p (n t) -> p n t", t=PACK), h_ps[:].rearrange("p t n -> p n t"), ACT.Relu)
-            nc.vector.quantize_mx(out=h_codes[:, cols].bitcast(FP8X4), scales=h_plane[:, cols], in_=h_bf[:, c % 2, :])
-            h_q.append((h_codes[:, cols], h_plane[:, cols]))
+                for part in range(2):
+                    entries = slice(HALF // LIST_ROWS * part, HALF // LIST_ROWS * (part + 1))
+                    nc.vector.tensor_copy(out=x_codes[:, HALF * part : HALF * (part + 1)], in_=x_tab[:].bitcast(U32).indirect(offs_sb[:, entries]))
+            h_codes = tile([P, HALF], U32, f"h_codes{half}", "x_tab" if half == 1 else None)
+            h_plane = tile([P, HALF], U8, f"h_plane{half}")
+            h_flat = h_bf[:].rearrange("p c n -> p (c n)")
+            for u0, u1 in ((0, HALF),) if half == 0 else ((0, P), (P, HALF)):
+                nc.vector.quantize_mx(out=h_codes[:, u0:u1].bitcast(FP8X4), scales=h_plane[:, u0:u1], in_=h_flat[:, PACK * u0 : PACK * u1])
+            h_q.extend((h_codes[:, P * c : P * (c + 1)], h_plane[:, P * c : P * (c + 1)]) for c in range(2))
 
-        for c in range(S // P):
-            users = slice(P * c, P * (c + 1))
-            for n0, n1 in ((0, V // 2), (V // 2, V)) if c == 0 else ((0, V),):
-                deep = (h_q[c][0], h_q[c][1], v_codes[:, n0:n1], v_plane[V_ROW:P, n0:n1])
-                wide = (x_codes[:, users], ex_plane[:, V + P * c : V + P * (c + 1)], e_codes[:, n0:n1], ex_plane[:, n0:n1])
+        pieces = [(0, 0, V // 2), (0, V // 2, V)] + [(c, 0, V) for c in range(1, S // P)]
+        for group in (pieces[:3], pieces[3:]):
+            passes = []
+            for c, n0, n1 in group:
+                deep = (h_q[c], (v_codes[:, n0:n1], planes[:, V + n0 : V + n1]))
+                wide = ((x_codes[:, P * c : P * (c + 1)], planes[:, 2 * V + P * c : 2 * V + P * (c + 1)]), (e_codes[:, n0:n1], planes[:, n0:n1]))
                 y_ps = psum.tile([P, n1 - n0], F32, name=f"y_ps{c}_{n0}", tag="h_ps0" if n0 > 0 else f"y_ps{c}")
-                for step, (user_codes, user_plane, item_codes, item_plane) in enumerate((deep, wide) if c < 2 else (wide, deep)):
-                    nc.tensor.matmul_mx(
-                        out=y_ps[:],
-                        lhsT=user_codes.bitcast(FP8X4),
-                        lhsT_scale=user_plane,
-                        rhs=item_codes.bitcast(FP8X4),
-                        rhs_scale=item_plane,
-                        start=(step == 0),
-                        stop=(step == 1),
-                    )
+                passes.append((y_ps, deep, wide) if c < 2 else (y_ps, wide, deep))
+            for y_ps, first, second in passes:
+                mx_pass(y_ps[:], first[0], first[1], True, False)
+            for (c, n0, n1), (y_ps, first, second) in zip(group, passes):
+                mx_pass(y_ps[:], second[0], second[1], False, True)
                 scores = tile([P, n1 - n0], F32, f"scores{c}_{n0}")
                 nc.scalar.activation(scores[:], y_ps[:], ACT.Sigmoid)
-                nc.sync.dma_start(out=out[users, n0:n1], in_=scores[:])
+                nc.sync.dma_start(out=out[P * c : P * (c + 1), n0:n1], in_=scores[:])

@@ -19,7 +19,8 @@ K, H = 512, 512
 T, W = 2048, 1024
 S, V = 512, 512
 HALF = 256
-W_FIRST = 2
+W_FIRST = 1
+M_SCALAR = 96
 FLOPS = 2 * K * H * S + 2 * K * S * V + 2 * H * S * V
 
 
@@ -44,6 +45,10 @@ def tile_picked_zwd_sigmoid_p_kernel(tc, x_words, x_scales, e_words, e_scales, v
         def load_scales(table, rows):
             nc.sync.dma_start(out=table[0:P:8, :].bitcast(I32), in_=rows[0].bitcast(I32))
 
+        def place_scales(plane, picked):
+            for r in range(4):
+                nc.sync.dma_start(out=plane[r:P:QUAD, :].bitcast(I32), in_=picked[8 * r : P : QUAD, :].bitcast(I32))
+
         def gather(window, dtype, offsets, n, name, reuse=None):
             picked = tile([P, n], dtype, name, reuse)
             nc.vector.tensor_copy(out=picked[:], in_=window[:].bitcast(dtype).indirect(offsets))
@@ -58,8 +63,9 @@ def tile_picked_zwd_sigmoid_p_kernel(tc, x_words, x_scales, e_words, e_scales, v
         es_tab = tile([P, W], U8, "es_tab")
         vs_tab = tile([P, W], U8, "vs_tab")
         xs_tab = tile([P, T], U8, "xs_tab")
-        planes = tile([P, 2 * V + S], U8, "planes")
-        for cleared in (es_tab, vs_tab, xs_tab, planes):
+        v_plane = tile([P, V], U8, "v_plane")
+        ex_plane = tile([P, V + S], U8, "ex_plane")
+        for cleared in (vs_tab, es_tab, xs_tab, v_plane, ex_plane):
             nc.vector.memset(cleared[:].bitcast(I32), 0)
 
         warm_in = tile([P, 1], F32, "warm_in")
@@ -72,39 +78,40 @@ def tile_picked_zwd_sigmoid_p_kernel(tc, x_words, x_scales, e_words, e_scales, v
         nc.sync.dma_start(out=w_raw[:, 0:W_FIRST, :], in_=w_rows[:, 0:W_FIRST, :])
         nc.sync.dma_start(cand_sb[:], cand)
         nc.sync.dma_start(offs_sb[:], offs)
-        load_scales(es_tab, e_scales)
         load_scales(vs_tab, v_scales)
+        load_scales(es_tab, e_scales)
         nc.sync.dma_start(out=w_raw[:, W_FIRST:PACK, :], in_=w_rows[:, W_FIRST:PACK, :])
         load_scales(xs_tab, x_scales)
         g_raw = tile([P, PACK, S], F32, "g_raw")
         nc.sync.dma_start(out=g_raw[:], in_=gT.rearrange("(p j) c -> p j c", j=PACK))
         e_tab = load_words(e_words, "e_tab")
-        v_tab = load_words(v_words, "v_tab")
-        x_tab = tile([P, T], I32, "x_tab")
-        x_rows = x_words[0].rearrange("p n t -> p (n t)").bitcast(I32)
-        nc.sync.dma_start(out=x_tab[:, 0 : T // 2], in_=x_rows[:, 0 : T // 2])
 
-        picked = tile([P, 2 * V + S], U8, "picked")
-        nc.vector.tensor_copy(out=picked[:, 0:V], in_=es_tab[:].indirect(cand_sb[:]))
-        nc.vector.tensor_copy(out=picked[:, V : 2 * V], in_=vs_tab[:].indirect(cand_sb[:]))
-        nc.vector.tensor_copy(out=picked[:, 2 * V : 2 * V + S], in_=xs_tab[:].indirect(offs_sb[:]))
-        for r in range(4):
-            nc.sync.dma_start(out=planes[r:P:QUAD, :].bitcast(I32), in_=picked[8 * r : P : QUAD, :].bitcast(I32))
-        nc.sync.dma_start(out=x_tab[:, T // 2 : T], in_=x_rows[:, T // 2 : T])
+        v_picked = gather(vs_tab, U8, cand_sb[:], V, "v_picked")
+        v_tab = load_words(v_words, "v_tab")
+        place_scales(v_plane, v_picked)
+        x_tab = load_words(x_words, "x_tab")
+        ex_picked = tile([P, V + S], U8, "ex_picked")
+        nc.vector.tensor_copy(out=ex_picked[:, 0:V], in_=es_tab[:].indirect(cand_sb[:]))
+        nc.vector.tensor_copy(out=ex_picked[:, V : V + S], in_=xs_tab[:].indirect(offs_sb[:]))
+        place_scales(ex_plane, ex_picked)
 
         w_bf = tile([P, H * PACK], BF16, "w_bf")
-        nc.scalar.copy(out=w_bf[:].rearrange("p (t m j) -> p m j t", t=PACK, j=PACK), in_=w_raw[:].rearrange("p j (m t) -> p m j t", t=PACK))
+        w_out = w_bf[:].rearrange("p (t m j) -> p m j t", t=PACK, j=PACK)
+        w_in = w_raw[:].rearrange("p j (m t) -> p m j t", t=PACK)
+        nc.scalar.copy(out=w_out[:, 0:M_SCALAR], in_=w_in[:, 0:M_SCALAR])
+        nc.vector.tensor_copy(out=w_out[:, M_SCALAR:P], in_=w_in[:, M_SCALAR:P])
         w_codes, w_plane = quantize(w_bf[:], H, "w")
 
         g_bf = tile([P, S * PACK], BF16, "g_bf")
         g_codes = tile([P, S], U32, "g_codes")
         g_plane = tile([P, S], U8, "g_plane")
         for c in range(S // P):
-            nc.scalar.copy(
+            cast = nc.vector.tensor_copy if c == 0 else nc.scalar.copy
+            cast(
                 out=g_bf[:, PACK * P * c : PACK * P * (c + 1)].rearrange("p (c i j) -> p c j i", i=4, j=PACK),
                 in_=g_raw[:, :, P * c : P * (c + 1)].rearrange("p j (c i) -> p c j i", i=4),
             )
-        for u0, u1 in ((0, P), (P, HALF), (HALF, S)):
+        for u0, u1 in ((0, HALF), (HALF, S)):
             nc.vector.quantize_mx(out=g_codes[:, u0:u1].bitcast(FP8X4), scales=g_plane[:, u0:u1], in_=g_bf[:, PACK * u0 : PACK * u1])
         e_codes = gather(e_tab, U32, cand_sb[:], V, "e_codes")
         v_codes = gather(v_tab, U32, cand_sb[:], V, "v_codes")
@@ -146,8 +153,8 @@ def tile_picked_zwd_sigmoid_p_kernel(tc, x_words, x_scales, e_words, e_scales, v
         for group in (pieces[:3], pieces[3:]):
             passes = []
             for c, n0, n1 in group:
-                deep = (h_q[c], (v_codes[:, n0:n1], planes[:, V + n0 : V + n1]))
-                wide = ((x_codes[:, P * c : P * (c + 1)], planes[:, 2 * V + P * c : 2 * V + P * (c + 1)]), (e_codes[:, n0:n1], planes[:, n0:n1]))
+                deep = (h_q[c], (v_codes[:, n0:n1], v_plane[:, n0:n1]))
+                wide = ((x_codes[:, P * c : P * (c + 1)], ex_plane[:, V + P * c : V + P * (c + 1)]), (e_codes[:, n0:n1], ex_plane[:, n0:n1]))
                 y_ps = psum.tile([P, n1 - n0], F32, name=f"y_ps{c}_{n0}", tag="h_ps0" if n0 > 0 else f"y_ps{c}")
                 passes.append((y_ps, deep, wide) if c < 2 else (y_ps, wide, deep))
             for y_ps, first, second in passes:

@@ -21,6 +21,7 @@ S, V = 512, 512
 HALF = 256
 W_FIRST = 1
 M_SCALAR = 96
+ITEM_ROW = 4
 FLOPS = 2 * K * H * S + 2 * K * S * V + 2 * H * S * V
 
 
@@ -45,9 +46,9 @@ def tile_picked_zwd_sigmoid_p_kernel(tc, x_words, x_scales, e_words, e_scales, v
         def load_scales(table, rows):
             nc.sync.dma_start(out=table[0:P:8, :].bitcast(I32), in_=rows[0].bitcast(I32))
 
-        def place_scales(plane, picked):
+        def place_scales(plane, picked, first_row):
             for r in range(4):
-                nc.sync.dma_start(out=plane[r:P:QUAD, :].bitcast(I32), in_=picked[8 * r : P : QUAD, :].bitcast(I32))
+                nc.sync.dma_start(out=plane[first_row + r : P : QUAD, :].bitcast(I32), in_=picked[8 * r : P : QUAD, :].bitcast(I32))
 
         def gather(window, dtype, offsets, n, name, reuse=None):
             picked = tile([P, n], dtype, name, reuse)
@@ -63,9 +64,9 @@ def tile_picked_zwd_sigmoid_p_kernel(tc, x_words, x_scales, e_words, e_scales, v
         es_tab = tile([P, W], U8, "es_tab")
         vs_tab = tile([P, W], U8, "vs_tab")
         xs_tab = tile([P, T], U8, "xs_tab")
-        v_plane = tile([P, V], U8, "v_plane")
-        ex_plane = tile([P, V + S], U8, "ex_plane")
-        for cleared in (vs_tab, es_tab, xs_tab, v_plane, ex_plane):
+        item_plane = tile([P, 2 * V], U8, "item_plane")
+        x_plane = tile([P, S], U8, "x_plane")
+        for cleared in (vs_tab, es_tab, xs_tab, item_plane, x_plane):
             nc.vector.memset(cleared[:].bitcast(I32), 0)
 
         warm_in = tile([P, 1], F32, "warm_in")
@@ -86,14 +87,13 @@ def tile_picked_zwd_sigmoid_p_kernel(tc, x_words, x_scales, e_words, e_scales, v
         nc.sync.dma_start(out=g_raw[:], in_=gT.rearrange("(p j) c -> p j c", j=PACK))
         e_tab = load_words(e_words, "e_tab")
 
-        v_picked = gather(vs_tab, U8, cand_sb[:], V, "v_picked")
+        item_picked = tile([P, 2 * V], U8, "item_picked")
+        nc.vector.tensor_copy(out=item_picked[:, 0:V], in_=vs_tab[:].indirect(cand_sb[:]))
+        nc.vector.tensor_copy(out=item_picked[:, V : 2 * V], in_=es_tab[:].indirect(cand_sb[:]))
         v_tab = load_words(v_words, "v_tab")
-        place_scales(v_plane, v_picked)
+        place_scales(item_plane, item_picked, ITEM_ROW)
         x_tab = load_words(x_words, "x_tab")
-        ex_picked = tile([P, V + S], U8, "ex_picked")
-        nc.vector.tensor_copy(out=ex_picked[:, 0:V], in_=es_tab[:].indirect(cand_sb[:]))
-        nc.vector.tensor_copy(out=ex_picked[:, V : V + S], in_=xs_tab[:].indirect(offs_sb[:]))
-        place_scales(ex_plane, ex_picked)
+        place_scales(x_plane, gather(xs_tab, U8, offs_sb[:], S, "x_picked"), 0)
 
         w_bf = tile([P, H * PACK], BF16, "w_bf")
         w_out = w_bf[:].rearrange("p (t m j) -> p m j t", t=PACK, j=PACK)
@@ -153,8 +153,8 @@ def tile_picked_zwd_sigmoid_p_kernel(tc, x_words, x_scales, e_words, e_scales, v
         for group in (pieces[:3], pieces[3:]):
             passes = []
             for c, n0, n1 in group:
-                deep = (h_q[c], (v_codes[:, n0:n1], v_plane[:, n0:n1]))
-                wide = ((x_codes[:, P * c : P * (c + 1)], ex_plane[:, V + P * c : V + P * (c + 1)]), (e_codes[:, n0:n1], ex_plane[:, n0:n1]))
+                deep = (h_q[c], (v_codes[:, n0:n1], item_plane[ITEM_ROW:P, n0:n1]))
+                wide = ((x_codes[:, P * c : P * (c + 1)], x_plane[:, P * c : P * (c + 1)]), (e_codes[:, n0:n1], item_plane[ITEM_ROW:P, V + n0 : V + n1]))
                 y_ps = psum.tile([P, n1 - n0], F32, name=f"y_ps{c}_{n0}", tag="h_ps0" if n0 > 0 else f"y_ps{c}")
                 passes.append((y_ps, deep, wide) if c < 2 else (y_ps, wide, deep))
             for y_ps, first, second in passes:

@@ -150,7 +150,7 @@ def tile_picked_zwd_sigmoid_p_kernel(tc, x_words, x_scales, e_words, e_scales, v
             h_q.extend((h_codes[:, P * c : P * (c + 1)], h_plane[:, P * c : P * (c + 1)]) for c in range(2))
 
         pieces = [(0, 0, V // 2), (0, V // 2, V)] + [(c, 0, V) for c in range(1, S // P)]
-        for group in (pieces[:3], pieces[3:]):
+        for group in (pieces[:3], pieces[3:4], pieces[4:]):
             passes = []
             for c, n0, n1 in group:
                 deep = (h_q[c], (v_codes[:, n0:n1], item_plane[ITEM_ROW:P, n0:n1]))

@@ -21,7 +21,7 @@ S, V = 512, 512
 HALF = 256
 W_FIRST = 1
 M_SCALAR = 96
-ITEM_ROW = 4
+V_ROW = 4
 FLOPS = 2 * K * H * S + 2 * K * S * V + 2 * H * S * V
 
 
@@ -43,12 +43,12 @@ def tile_picked_zwd_sigmoid_p_kernel(tc, x_words, x_scales, e_words, e_scales, v
             nc.sync.dma_start(out=table[:], in_=words[0].rearrange("p n t -> p (n t)").bitcast(I32))
             return table
 
-        def load_scales(table, rows):
-            nc.sync.dma_start(out=table[0:P:8, :].bitcast(I32), in_=rows[0].bitcast(I32))
+        def load_scales(table, rows, first_row):
+            nc.sync.dma_start(out=table[first_row:P:8, :].bitcast(I32), in_=rows[0].bitcast(I32))
 
         def place_scales(plane, picked, first_row):
             for r in range(4):
-                nc.sync.dma_start(out=plane[first_row + r : P : QUAD, :].bitcast(I32), in_=picked[8 * r : P : QUAD, :].bitcast(I32))
+                nc.sync.dma_start(out=plane[first_row + r : P : QUAD, :].bitcast(I32), in_=picked[first_row + 8 * r : P : QUAD, :].bitcast(I32))
 
         def gather(window, dtype, offsets, n, name, reuse=None):
             picked = tile([P, n], dtype, name, reuse)
@@ -64,9 +64,9 @@ def tile_picked_zwd_sigmoid_p_kernel(tc, x_words, x_scales, e_words, e_scales, v
         es_tab = tile([P, W], U8, "es_tab")
         vs_tab = tile([P, W], U8, "vs_tab")
         xs_tab = tile([P, T], U8, "xs_tab")
-        item_plane = tile([P, 2 * V], U8, "item_plane")
-        x_plane = tile([P, S], U8, "x_plane")
-        for cleared in (vs_tab, es_tab, xs_tab, item_plane, x_plane):
+        v_plane = tile([P, V], U8, "v_plane")
+        ex_plane = tile([P, V + S], U8, "ex_plane")
+        for cleared in (vs_tab, es_tab, xs_tab, v_plane, ex_plane):
             nc.vector.memset(cleared[:].bitcast(I32), 0)
 
         warm_in = tile([P, 1], F32, "warm_in")
@@ -79,21 +79,22 @@ def tile_picked_zwd_sigmoid_p_kernel(tc, x_words, x_scales, e_words, e_scales, v
         nc.sync.dma_start(out=w_raw[:, 0:W_FIRST, :], in_=w_rows[:, 0:W_FIRST, :])
         nc.sync.dma_start(cand_sb[:], cand)
         nc.sync.dma_start(offs_sb[:], offs)
-        load_scales(vs_tab, v_scales)
-        load_scales(es_tab, e_scales)
+        load_scales(vs_tab, v_scales, V_ROW)
+        load_scales(es_tab, e_scales, 0)
         nc.sync.dma_start(out=w_raw[:, W_FIRST:PACK, :], in_=w_rows[:, W_FIRST:PACK, :])
-        load_scales(xs_tab, x_scales)
+        load_scales(xs_tab, x_scales, 0)
         g_raw = tile([P, PACK, S], F32, "g_raw")
         nc.sync.dma_start(out=g_raw[:], in_=gT.rearrange("(p j) c -> p j c", j=PACK))
         e_tab = load_words(e_words, "e_tab")
 
-        item_picked = tile([P, 2 * V], U8, "item_picked")
-        nc.vector.tensor_copy(out=item_picked[:, 0:V], in_=vs_tab[:].indirect(cand_sb[:]))
-        nc.vector.tensor_copy(out=item_picked[:, V : 2 * V], in_=es_tab[:].indirect(cand_sb[:]))
+        v_picked = gather(vs_tab, U8, cand_sb[:], V, "v_picked")
         v_tab = load_words(v_words, "v_tab")
-        place_scales(item_plane, item_picked, ITEM_ROW)
+        place_scales(v_plane, v_picked, V_ROW)
         x_tab = load_words(x_words, "x_tab")
-        place_scales(x_plane, gather(xs_tab, U8, offs_sb[:], S, "x_picked"), 0)
+        ex_picked = tile([P, V + S], U8, "ex_picked")
+        nc.vector.tensor_copy(out=ex_picked[:, 0:V], in_=es_tab[:].indirect(cand_sb[:]))
+        nc.vector.tensor_copy(out=ex_picked[:, V : V + S], in_=xs_tab[:].indirect(offs_sb[:]))
+        place_scales(ex_plane, ex_picked, 0)
 
         w_bf = tile([P, H * PACK], BF16, "w_bf")
         w_out = w_bf[:].rearrange("p (t m j) -> p m j t", t=PACK, j=PACK)
@@ -153,8 +154,8 @@ def tile_picked_zwd_sigmoid_p_kernel(tc, x_words, x_scales, e_words, e_scales, v
         for group in (pieces[:3], pieces[3:4], pieces[4:]):
             passes = []
             for c, n0, n1 in group:
-                deep = (h_q[c], (v_codes[:, n0:n1], item_plane[ITEM_ROW:P, n0:n1]))
-                wide = ((x_codes[:, P * c : P * (c + 1)], x_plane[:, P * c : P * (c + 1)]), (e_codes[:, n0:n1], item_plane[ITEM_ROW:P, V + n0 : V + n1]))
+                deep = (h_q[c], (v_codes[:, n0:n1], v_plane[V_ROW:P, n0:n1]))
+                wide = ((x_codes[:, P * c : P * (c + 1)], ex_plane[:, V + P * c : V + P * (c + 1)]), (e_codes[:, n0:n1], ex_plane[:, n0:n1]))
                 y_ps = psum.tile([P, n1 - n0], F32, name=f"y_ps{c}_{n0}", tag="h_ps0" if n0 > 0 else f"y_ps{c}")
                 passes.append((y_ps, deep, wide) if c < 2 else (y_ps, wide, deep))
             for y_ps, first, second in passes:

@@ -129,6 +129,16 @@ def tile_picked_zwd_sigmoid_p_kernel(tc, x_words, x_scales, e_words, e_scales, v
             )
 
         h_q = []
+        x_q = []
+
+        def gather_users(half, reuse):
+            x_codes = tile([P, HALF], U32, f"x_codes{half}", reuse)
+            for c in range(2):
+                tile_c = 2 * half + c
+                entries = slice(P // LIST_ROWS * tile_c, P // LIST_ROWS * (tile_c + 1))
+                nc.vector.tensor_copy(out=x_codes[:, P * c : P * (c + 1)], in_=x_tab[:].bitcast(U32).indirect(offs_sb[:, entries]))
+                x_q.append((x_codes[:, P * c : P * (c + 1)], ex_plane[:, V + P * tile_c : V + P * (tile_c + 1)]))
+
         for half in range(2):
             h_bf = tile([P, 2, P * PACK], BF16, f"h_bf{half}")
             for c in (2 * half, 2 * half + 1):
@@ -139,25 +149,22 @@ def tile_picked_zwd_sigmoid_p_kernel(tc, x_words, x_scales, e_words, e_scales, v
                     mx_pass(h_ps[:, t, :], (w_codes[:, channels], w_plane[:, channels]), (g_codes[:, users], g_plane[:, users]), True, True)
                 nc.scalar.activation(h_bf[:, c % 2, :].rearrange("p (n t) -> p n t", t=PACK), h_ps[:].rearrange("p t n -> p n t"), ACT.Relu)
             if half == 1:
-                x_codes = tile([P, S], U32, "x_codes")
-                for part in range(2):
-                    entries = slice(HALF // LIST_ROWS * part, HALF // LIST_ROWS * (part + 1))
-                    nc.vector.tensor_copy(out=x_codes[:, HALF * part : HALF * (part + 1)], in_=x_tab[:].bitcast(U32).indirect(offs_sb[:, entries]))
-            h_codes = tile([P, HALF], U32, f"h_codes{half}", "x_tab" if half == 1 else None)
+                gather_users(0, None)
+            h_codes = tile([P, HALF], U32, f"h_codes{half}", "ex_picked" if half == 1 else None)
             h_plane = tile([P, HALF], U8, f"h_plane{half}")
-            h_flat = h_bf[:].rearrange("p c n -> p (c n)")
-            for u0, u1 in ((0, HALF),) if half == 0 else ((0, P), (P, HALF)):
-                nc.vector.quantize_mx(out=h_codes[:, u0:u1].bitcast(FP8X4), scales=h_plane[:, u0:u1], in_=h_flat[:, PACK * u0 : PACK * u1])
+            nc.vector.quantize_mx(out=h_codes[:].bitcast(FP8X4), scales=h_plane[:], in_=h_bf[:].rearrange("p c n -> p (c n)"))
+            if half == 1:
+                gather_users(1, "h_bf1")
             h_q.extend((h_codes[:, P * c : P * (c + 1)], h_plane[:, P * c : P * (c + 1)]) for c in range(2))
 
         pieces = [(0, 0, V // 2), (0, V // 2, V)] + [(c, 0, V) for c in range(1, S // P)]
-        for group in (pieces[:3], pieces[3:4], pieces[4:]):
+        for group in (pieces[:3], pieces[3:]):
             passes = []
             for c, n0, n1 in group:
                 deep = (h_q[c], (v_codes[:, n0:n1], v_plane[V_ROW:P, n0:n1]))
-                wide = ((x_codes[:, P * c : P * (c + 1)], ex_plane[:, V + P * c : V + P * (c + 1)]), (e_codes[:, n0:n1], ex_plane[:, n0:n1]))
+                wide = (x_q[c], (e_codes[:, n0:n1], ex_plane[:, n0:n1]))
                 y_ps = psum.tile([P, n1 - n0], F32, name=f"y_ps{c}_{n0}", tag="h_ps0" if n0 > 0 else f"y_ps{c}")
-                passes.append((y_ps, deep, wide) if c < 2 else (y_ps, wide, deep))
+                passes.append((y_ps, deep, wide))
             for y_ps, first, second in passes:
                 mx_pass(y_ps[:], first[0], first[1], True, False)
             for (c, n0, n1), (y_ps, first, second) in zip(group, passes):

@@ -128,47 +128,44 @@ def tile_picked_zwd_sigmoid_p_kernel(tc, x_words, x_scales, e_words, e_scales, v
                 stop=stop,
             )
 
+        def hidden(c, h_bf):
+            users = slice(P * c, P * (c + 1))
+            h_ps = psum.tile([P, PACK, P], F32, name=f"h_ps{c}", tag=f"h_ps{c}")
+            for t in range(PACK):
+                channels = slice(P * t, P * (t + 1))
+                mx_pass(h_ps[:, t, :], (w_codes[:, channels], w_plane[:, channels]), (g_codes[:, users], g_plane[:, users]), True, True)
+            nc.scalar.activation(h_bf.rearrange("p (n t) -> p n t", t=PACK), h_ps[:].rearrange("p t n -> p n t"), ACT.Relu)
+
+        def quantize_hidden(h_bf, n, name, reuse=None):
+            codes = tile([P, n], U32, name + "_codes", reuse)
+            plane = tile([P, n], U8, name + "_plane")
+            nc.vector.quantize_mx(out=codes[:].bitcast(FP8X4), scales=plane[:], in_=h_bf)
+            return [(codes[:, u : u + P], plane[:, u : u + P]) for u in range(0, n, P)]
+
+        def gather_part(table, offsets, first, n, name, reuse=None):
+            return gather(table, U32, offsets[:, first // LIST_ROWS : (first + n) // LIST_ROWS], n, name, reuse)
+
         h_q = []
-        x_q = []
-
-        def gather_users(half, reuse):
-            x_codes = tile([P, HALF], U32, f"x_codes{half}", reuse)
-            for c in range(2):
-                tile_c = 2 * half + c
-                entries = slice(P // LIST_ROWS * tile_c, P // LIST_ROWS * (tile_c + 1))
-                nc.vector.tensor_copy(out=x_codes[:, P * c : P * (c + 1)], in_=x_tab[:].bitcast(U32).indirect(offs_sb[:, entries]))
-                x_q.append((x_codes[:, P * c : P * (c + 1)], ex_plane[:, V + P * tile_c : V + P * (tile_c + 1)]))
-
+        x_codes = []
         for half in range(2):
-            h_bf = tile([P, 2, P * PACK], BF16, f"h_bf{half}")
-            for c in (2 * half, 2 * half + 1):
-                users = slice(P * c, P * (c + 1))
-                h_ps = psum.tile([P, PACK, P], F32, name=f"h_ps{c}", tag=f"h_ps{c}")
-                for t in range(PACK):
-                    channels = slice(P * t, P * (t + 1))
-                    mx_pass(h_ps[:, t, :], (w_codes[:, channels], w_plane[:, channels]), (g_codes[:, users], g_plane[:, users]), True, True)
-                nc.scalar.activation(h_bf[:, c % 2, :].rearrange("p (n t) -> p n t", t=PACK), h_ps[:].rearrange("p t n -> p n t"), ACT.Relu)
-            if half == 1:
-                gather_users(0, None)
-            h_codes = tile([P, HALF], U32, f"h_codes{half}", "ex_picked" if half == 1 else None)
-            h_plane = tile([P, HALF], U8, f"h_plane{half}")
-            nc.vector.quantize_mx(out=h_codes[:].bitcast(FP8X4), scales=h_plane[:], in_=h_bf[:].rearrange("p c n -> p (c n)"))
-            if half == 1:
-                gather_users(1, "h_bf1")
-            h_q.extend((h_codes[:, P * c : P * (c + 1)], h_plane[:, P * c : P * (c + 1)]) for c in range(2))
+            h_bf = tile([P, 2 * P * PACK], BF16, f"h_bf{half}")
+            for c in range(2):
+                hidden(2 * half + c, h_bf[:, P * PACK * c : P * PACK * (c + 1)])
+            if half == 0:
+                h_q.extend(quantize_hidden(h_bf[:], HALF, "h0"))
+            else:
+                x_codes.extend(gather_part(x_tab, offs_sb, P * c, P, f"x_codes{c}") for c in range(3))
+                h_q.extend(quantize_hidden(h_bf[:], HALF, "h1", "ex_picked"))
+                x_codes.append(gather_part(x_tab, offs_sb, P * 3, P, "x_codes3", "h_bf1"))
 
-        pieces = [(0, 0, V // 2), (0, V // 2, V)] + [(c, 0, V) for c in range(1, S // P)]
-        for group in (pieces[:3], pieces[3:]):
-            passes = []
-            for c, n0, n1 in group:
-                deep = (h_q[c], (v_codes[:, n0:n1], v_plane[V_ROW:P, n0:n1]))
-                wide = (x_q[c], (e_codes[:, n0:n1], ex_plane[:, n0:n1]))
-                y_ps = psum.tile([P, n1 - n0], F32, name=f"y_ps{c}_{n0}", tag="h_ps0" if n0 > 0 else f"y_ps{c}")
-                passes.append((y_ps, deep, wide))
-            for y_ps, first, second in passes:
-                mx_pass(y_ps[:], first[0], first[1], True, False)
-            for (c, n0, n1), (y_ps, first, second) in zip(group, passes):
-                mx_pass(y_ps[:], second[0], second[1], False, True)
-                scores = tile([P, n1 - n0], F32, f"scores{c}_{n0}")
-                nc.scalar.activation(scores[:], y_ps[:], ACT.Sigmoid)
-                nc.sync.dma_start(out=out[P * c : P * (c + 1), n0:n1], in_=scores[:])
+        pieces = [(0, 0, HALF), (0, HALF, V)] + [(c, 0, V) for c in range(1, S // P)]
+        for c, n0, n1 in pieces:
+            y_ps = psum.tile([P, n1 - n0], F32, name=f"y_ps{c}_{n0}", tag="h_ps0" if n0 > 0 else f"y_ps{c}")
+            deep = (h_q[c], (v_codes[:, n0:n1], v_plane[V_ROW:P, n0:n1]))
+            wide = ((x_codes[c][:], ex_plane[:, V + P * c : V + P * (c + 1)]), (e_codes[:, n0:n1], ex_plane[:, n0:n1]))
+            first, second = (wide, deep) if c == 2 else (deep, wide)
+            mx_pass(y_ps[:], first[0], first[1], True, False)
+            mx_pass(y_ps[:], second[0], second[1], False, True)
+            scores = tile([P, n1 - n0], F32, f"scores{c}_{n0}")
+            nc.scalar.activation(scores[:], y_ps[:], ACT.Sigmoid)
+            nc.sync.dma_start(out=out[P * c : P * (c + 1), n0:n1], in_=scores[:])

@@ -19,8 +19,8 @@ K, H = 512, 512
 T, W = 2048, 1024
 S, V = 512, 512
 HALF = 256
-W_FIRST = 1
-M_SCALAR = 96
+W_FIRST = 512
+M_SCALAR = 92
 V_ROW = 4
 FLOPS = 2 * K * H * S + 2 * K * S * V + 2 * H * S * V
 
@@ -66,7 +66,8 @@ def tile_picked_zwd_sigmoid_p_kernel(tc, x_words, x_scales, e_words, e_scales, v
         xs_tab = tile([P, T], U8, "xs_tab")
         v_plane = tile([P, V], U8, "v_plane")
         ex_plane = tile([P, V + S], U8, "ex_plane")
-        for cleared in (vs_tab, es_tab, xs_tab, v_plane, ex_plane):
+        nc.gpsimd.memset(es_tab[:].bitcast(I32), 0)
+        for cleared in (vs_tab, xs_tab, v_plane, ex_plane):
             nc.vector.memset(cleared[:].bitcast(I32), 0)
 
         warm_in = tile([P, 1], F32, "warm_in")
@@ -75,13 +76,14 @@ def tile_picked_zwd_sigmoid_p_kernel(tc, x_words, x_scales, e_words, e_scales, v
         nc.scalar.activation(warm_out[:], warm_in[:], ACT.Sigmoid)
 
         w_raw = tile([P, PACK, H], F32, "w_raw")
-        w_rows = w1.rearrange("(p j) c -> p j c", j=PACK)
-        nc.sync.dma_start(out=w_raw[:, 0:W_FIRST, :], in_=w_rows[:, 0:W_FIRST, :])
+        w_flat = w_raw[:].rearrange("p j c -> p (j c)")
+        w_rows = w1.rearrange("(p j) c -> p (j c)", j=PACK)
+        nc.sync.dma_start(out=w_flat[:, 0:W_FIRST], in_=w_rows[:, 0:W_FIRST])
         nc.sync.dma_start(cand_sb[:], cand)
-        nc.sync.dma_start(offs_sb[:], offs)
         load_scales(vs_tab, v_scales, V_ROW)
         load_scales(es_tab, e_scales, 0)
-        nc.sync.dma_start(out=w_raw[:, W_FIRST:PACK, :], in_=w_rows[:, W_FIRST:PACK, :])
+        nc.sync.dma_start(out=w_flat[:, W_FIRST : PACK * H], in_=w_rows[:, W_FIRST : PACK * H])
+        nc.sync.dma_start(offs_sb[:], offs)
         load_scales(xs_tab, x_scales, 0)
         g_raw = tile([P, PACK, S], F32, "g_raw")
         nc.sync.dma_start(out=g_raw[:], in_=gT.rearrange("(p j) c -> p j c", j=PACK))
@@ -106,13 +108,13 @@ def tile_picked_zwd_sigmoid_p_kernel(tc, x_words, x_scales, e_words, e_scales, v
         g_bf = tile([P, S * PACK], BF16, "g_bf")
         g_codes = tile([P, S], U32, "g_codes")
         g_plane = tile([P, S], U8, "g_plane")
-        for c in range(S // P):
-            cast = nc.vector.tensor_copy if c == 0 else nc.scalar.copy
+        shares = [(nc.vector.tensor_copy, 0, P // 2), (nc.scalar.copy, P // 2, P), (nc.vector.tensor_copy, P, 3 * P // 2), (nc.scalar.copy, 3 * P // 2, HALF)]
+        for cast, u0, u1 in shares + [(nc.scalar.copy, HALF, HALF + P), (nc.scalar.copy, HALF + P, S)]:
             cast(
-                out=g_bf[:, PACK * P * c : PACK * P * (c + 1)].rearrange("p (c i j) -> p c j i", i=4, j=PACK),
-                in_=g_raw[:, :, P * c : P * (c + 1)].rearrange("p j (c i) -> p c j i", i=4),
+                out=g_bf[:, PACK * u0 : PACK * u1].rearrange("p (c i j) -> p c j i", i=4, j=PACK),
+                in_=g_raw[:, :, u0:u1].rearrange("p j (c i) -> p c j i", i=4),
             )
-        for u0, u1 in ((0, HALF), (HALF, S)):
+        for u0, u1 in ((0, P), (P, HALF), (HALF, S)):
             nc.vector.quantize_mx(out=g_codes[:, u0:u1].bitcast(FP8X4), scales=g_plane[:, u0:u1], in_=g_bf[:, PACK * u0 : PACK * u1])
         e_codes = gather(e_tab, U32, cand_sb[:], V, "e_codes")
         v_codes = gather(v_tab, U32, cand_sb[:], V, "v_codes")
@@ -136,27 +138,28 @@ def tile_picked_zwd_sigmoid_p_kernel(tc, x_words, x_scales, e_words, e_scales, v
                 mx_pass(h_ps[:, t, :], (w_codes[:, channels], w_plane[:, channels]), (g_codes[:, users], g_plane[:, users]), True, True)
             nc.scalar.activation(h_bf.rearrange("p (n t) -> p n t", t=PACK), h_ps[:].rearrange("p t n -> p n t"), ACT.Relu)
 
-        def quantize_hidden(h_bf, n, name, reuse=None):
-            codes = tile([P, n], U32, name + "_codes", reuse)
-            plane = tile([P, n], U8, name + "_plane")
-            nc.vector.quantize_mx(out=codes[:].bitcast(FP8X4), scales=plane[:], in_=h_bf)
-            return [(codes[:, u : u + P], plane[:, u : u + P]) for u in range(0, n, P)]
+        def quantize_hidden(sources, name, reuse=None):
+            codes = tile([P, HALF], U32, name + "_codes", reuse)
+            plane = tile([P, HALF], U8, name + "_plane")
+            width = HALF // len(sources)
+            for k, source in enumerate(sources):
+                users = slice(width * k, width * (k + 1))
+                nc.vector.quantize_mx(out=codes[:, users].bitcast(FP8X4), scales=plane[:, users], in_=source[:])
+            return [(codes[:, u : u + P], plane[:, u : u + P]) for u in (0, P)]
 
         def gather_part(table, offsets, first, n, name, reuse=None):
             return gather(table, U32, offsets[:, first // LIST_ROWS : (first + n) // LIST_ROWS], n, name, reuse)
 
-        h_q = []
-        x_codes = []
-        for half in range(2):
-            h_bf = tile([P, 2 * P * PACK], BF16, f"h_bf{half}")
-            for c in range(2):
-                hidden(2 * half + c, h_bf[:, P * PACK * c : P * PACK * (c + 1)])
-            if half == 0:
-                h_q.extend(quantize_hidden(h_bf[:], HALF, "h0"))
-            else:
-                x_codes.extend(gather_part(x_tab, offs_sb, P * c, P, f"x_codes{c}") for c in range(3))
-                h_q.extend(quantize_hidden(h_bf[:], HALF, "h1", "ex_picked"))
-                x_codes.append(gather_part(x_tab, offs_sb, P * 3, P, "x_codes3", "h_bf1"))
+        h_early = tile([P, 2 * P * PACK], BF16, "h_early")
+        for c in range(2):
+            hidden(c, h_early[:, P * PACK * c : P * PACK * (c + 1)])
+        h_q = quantize_hidden([h_early], "h_early")
+        h_late = [tile([P, P * PACK], BF16, f"h_bf{c}") for c in (2, 3)]
+        for c in (2, 3):
+            hidden(c, h_late[c - 2][:])
+        x_codes = [gather_part(x_tab, offs_sb, P * c, P, f"x_codes{c}") for c in range(3)]
+        h_q.extend(quantize_hidden(h_late, "h_late", "ex_picked"))
+        x_codes.append(gather_part(x_tab, offs_sb, P * 3, P, "x_codes3", "h_bf2"))
 
         pieces = [(0, 0, HALF), (0, HALF, V)] + [(c, 0, V) for c in range(1, S // P)]
         for c, n0, n1 in pieces:

@@ -20,7 +20,7 @@ T, W = 2048, 1024
 S, V = 512, 512
 HALF = 256
 W_FIRST = 512
-M_SCALAR = 92
+M_SCALAR = 84
 V_ROW = 4
 FLOPS = 2 * K * H * S + 2 * K * S * V + 2 * H * S * V
 
@@ -102,7 +102,14 @@ def tile_picked_zwd_sigmoid_p_kernel(tc, x_words, x_scales, e_words, e_scales, v
         w_out = w_bf[:].rearrange("p (t m j) -> p m j t", t=PACK, j=PACK)
         w_in = w_raw[:].rearrange("p j (m t) -> p m j t", t=PACK)
         nc.scalar.copy(out=w_out[:, 0:M_SCALAR], in_=w_in[:, 0:M_SCALAR])
-        nc.vector.tensor_copy(out=w_out[:, M_SCALAR:P], in_=w_in[:, M_SCALAR:P])
+        nc.gpsimd.tensor_scalar(
+            w_bf[:].rearrange("p (t m j) -> p m t j", t=PACK, j=PACK)[:, M_SCALAR:P],
+            w_raw[:].rearrange("p j (m t) -> p m t j", t=PACK)[:, M_SCALAR:P],
+            1.0,
+            0.0,
+            mybir.AluOpType.mult,
+            mybir.AluOpType.add,
+        )
         w_codes, w_plane = quantize(w_bf[:], H, "w")
 
         g_bf = tile([P, S * PACK], BF16, "g_bf")

@@ -19,7 +19,7 @@ K, H = 512, 512
 T, W = 2048, 1024
 S, V = 512, 512
 HALF = 256
-W_FIRST = 512
+W_FIRST = 1024
 M_SCALAR = 84
 V_ROW = 4
 FLOPS = 2 * K * H * S + 2 * K * S * V + 2 * H * S * V
@@ -66,8 +66,7 @@ def tile_picked_zwd_sigmoid_p_kernel(tc, x_words, x_scales, e_words, e_scales, v
         xs_tab = tile([P, T], U8, "xs_tab")
         v_plane = tile([P, V], U8, "v_plane")
         ex_plane = tile([P, V + S], U8, "ex_plane")
-        nc.gpsimd.memset(es_tab[:].bitcast(I32), 0)
-        for cleared in (vs_tab, xs_tab, v_plane, ex_plane):
+        for cleared in (vs_tab, es_tab, xs_tab, v_plane, ex_plane):
             nc.vector.memset(cleared[:].bitcast(I32), 0)
 
         warm_in = tile([P, 1], F32, "warm_in")
@@ -82,9 +81,9 @@ def tile_picked_zwd_sigmoid_p_kernel(tc, x_words, x_scales, e_words, e_scales, v
         nc.sync.dma_start(cand_sb[:], cand)
         load_scales(vs_tab, v_scales, V_ROW)
         load_scales(es_tab, e_scales, 0)
-        nc.sync.dma_start(out=w_flat[:, W_FIRST : PACK * H], in_=w_rows[:, W_FIRST : PACK * H])
         nc.sync.dma_start(offs_sb[:], offs)
         load_scales(xs_tab, x_scales, 0)
+        nc.sync.dma_start(out=w_flat[:, W_FIRST : PACK * H], in_=w_rows[:, W_FIRST : PACK * H])
         g_raw = tile([P, PACK, S], F32, "g_raw")
         nc.sync.dma_start(out=g_raw[:], in_=gT.rearrange("(p j) c -> p j c", j=PACK))
         e_tab = load_words(e_words, "e_tab")

@@ -114,8 +114,8 @@ def tile_picked_zwd_sigmoid_p_kernel(tc, x_words, x_scales, e_words, e_scales, v
         g_bf = tile([P, S * PACK], BF16, "g_bf")
         g_codes = tile([P, S], U32, "g_codes")
         g_plane = tile([P, S], U8, "g_plane")
-        shares = [(nc.vector.tensor_copy, 0, P // 2), (nc.scalar.copy, P // 2, P), (nc.vector.tensor_copy, P, 3 * P // 2), (nc.scalar.copy, 3 * P // 2, HALF)]
-        for cast, u0, u1 in shares + [(nc.scalar.copy, HALF, HALF + P), (nc.scalar.copy, HALF + P, S)]:
+        shares = [(nc.scalar.copy, 0, P), (nc.vector.tensor_copy, P, 3 * P // 2), (nc.scalar.copy, 3 * P // 2, HALF), (nc.scalar.copy, HALF, HALF + P), (nc.scalar.copy, HALF + P, S)]
+        for cast, u0, u1 in shares:
             cast(
                 out=g_bf[:, PACK * u0 : PACK * u1].rearrange("p (c i j) -> p c j i", i=4, j=PACK),
                 in_=g_raw[:, :, u0:u1].rearrange("p j (c i) -> p c j i", i=4),

@@ -156,10 +156,10 @@ def tile_picked_zwd_sigmoid_p_kernel(tc, x_words, x_scales, e_words, e_scales, v
         def gather_part(table, offsets, first, n, name, reuse=None):
             return gather(table, U32, offsets[:, first // LIST_ROWS : (first + n) // LIST_ROWS], n, name, reuse)
 
-        h_early = tile([P, 2 * P * PACK], BF16, "h_early")
-        for c in range(2):
-            hidden(c, h_early[:, P * PACK * c : P * PACK * (c + 1)])
-        h_q = quantize_hidden([h_early], "h_early")
+        h_early = [tile([P, P * PACK], BF16, f"h_bf{c}") for c in (0, 1)]
+        for c in (0, 1):
+            hidden(c, h_early[c][:])
+        h_q = quantize_hidden(h_early, "h_early")
         h_late = [tile([P, P * PACK], BF16, f"h_bf{c}") for c in (2, 3)]
         for c in (2, 3):
             hidden(c, h_late[c - 2][:])

@@ -19,7 +19,6 @@ K, H = 512, 512
 T, W = 2048, 1024
 S, V = 512, 512
 HALF = 256
-W_FIRST = 1024
 M_SCALAR = 84
 V_ROW = 4
 FLOPS = 2 * K * H * S + 2 * K * S * V + 2 * H * S * V
@@ -77,13 +76,13 @@ def tile_picked_zwd_sigmoid_p_kernel(tc, x_words, x_scales, e_words, e_scales, v
         w_raw = tile([P, PACK, H], F32, "w_raw")
         w_flat = w_raw[:].rearrange("p j c -> p (j c)")
         w_rows = w1.rearrange("(p j) c -> p (j c)", j=PACK)
-        nc.sync.dma_start(out=w_flat[:, 0:W_FIRST], in_=w_rows[:, 0:W_FIRST])
+        nc.sync.dma_start(out=w_flat[0:P:2, :], in_=w_rows[0:P:2, :])
         nc.sync.dma_start(cand_sb[:], cand)
         load_scales(vs_tab, v_scales, V_ROW)
         load_scales(es_tab, e_scales, 0)
         nc.sync.dma_start(offs_sb[:], offs)
         load_scales(xs_tab, x_scales, 0)
-        nc.sync.dma_start(out=w_flat[:, W_FIRST : PACK * H], in_=w_rows[:, W_FIRST : PACK * H])
+        nc.sync.dma_start(out=w_flat[1:P:2, :], in_=w_rows[1:P:2, :])
         g_raw = tile([P, PACK, S], F32, "g_raw")
         nc.sync.dma_start(out=g_raw[:], in_=gT.rearrange("(p j) c -> p j c", j=PACK))
         e_tab = load_words(e_words, "e_tab")

@@ -135,6 +135,9 @@ def tile_picked_zwd_sigmoid_p_kernel(tc, x_words, x_scales, e_words, e_scales, v
                 stop=stop,
             )
 
+        warm_ps = psum.tile([P, H], F32, name="warm_ps", tag="y_ps3")
+        mx_pass(warm_ps[:], (w_codes[:, 0:P], w_plane[:, 0:P]), (w_codes[:], w_plane[:]), True, True)
+
         def hidden(c, h_bf):
             users = slice(P * c, P * (c + 1))
             h_ps = psum.tile([P, PACK, P], F32, name=f"h_ps{c}", tag=f"h_ps{c}")

@@ -35,7 +35,7 @@ def tile_picked_zwd_sigmoid_p_kernel(tc, x_words, x_scales, e_words, e_scales, v
         cand_sb = lists.tile([P, V // LIST_ROWS], U16, name="cand_sb")
 
         def tile(shape, dtype, name, reuse=None):
-            return sb.tile(shape, dtype, name=name, tag=reuse or name, align_bytes=64)
+            return sb.tile(shape, dtype, name=name, tag=reuse or name, align_bytes=256)
 
         def load_words(words, name):
             table = tile([P, words.shape[2]], I32, name)

@@ -68,21 +68,22 @@ def tile_picked_zwd_sigmoid_p_kernel(tc, x_words, x_scales, e_words, e_scales, v
         for cleared in (vs_tab, es_tab, xs_tab, v_plane, ex_plane):
             nc.vector.memset(cleared[:].bitcast(I32), 0)
 
-        warm_in = tile([P, 1], F32, "warm_in")
-        warm_out = tile([P, 1], F32, "warm_out")
-        nc.gpsimd.memset(warm_in[:], 0.0)
-        nc.scalar.activation(warm_out[:], warm_in[:], ACT.Sigmoid)
-
         w_raw = tile([P, PACK, H], F32, "w_raw")
         w_flat = w_raw[:].rearrange("p j c -> p (j c)")
         w_rows = w1.rearrange("(p j) c -> p (j c)", j=PACK)
-        nc.sync.dma_start(out=w_flat[0:P:2, :], in_=w_rows[0:P:2, :])
+        nc.scalar.dma_start(out=w_flat[0:P:2, :], in_=w_rows[0:P:2, :])
         nc.sync.dma_start(cand_sb[:], cand)
         load_scales(vs_tab, v_scales, V_ROW)
         load_scales(es_tab, e_scales, 0)
         nc.sync.dma_start(offs_sb[:], offs)
         load_scales(xs_tab, x_scales, 0)
         nc.sync.dma_start(out=w_flat[1:P:2, :], in_=w_rows[1:P:2, :])
+
+        warm_in = tile([P, 1], F32, "warm_in")
+        warm_out = tile([P, 1], F32, "warm_out")
+        nc.gpsimd.memset(warm_in[:], 0.0)
+        nc.scalar.activation(warm_out[:], warm_in[:], ACT.Sigmoid)
+
         g_raw = tile([P, PACK, S], F32, "g_raw")
         nc.sync.dma_start(out=g_raw[:], in_=gT.rearrange("(p j) c -> p j c", j=PACK))
         e_tab = load_words(e_words, "e_tab")

@@ -73,9 +73,9 @@ def tile_picked_zwd_sigmoid_p_kernel(tc, x_words, x_scales, e_words, e_scales, v
         w_rows = w1.rearrange("(p j) c -> p (j c)", j=PACK)
         nc.scalar.dma_start(out=w_flat[0:P:2, :], in_=w_rows[0:P:2, :])
         nc.sync.dma_start(cand_sb[:], cand)
+        nc.sync.dma_start(offs_sb[:], offs)
         load_scales(vs_tab, v_scales, V_ROW)
         load_scales(es_tab, e_scales, 0)
-        nc.sync.dma_start(offs_sb[:], offs)
         load_scales(xs_tab, x_scales, 0)
         nc.sync.dma_start(out=w_flat[1:P:2, :], in_=w_rows[1:P:2, :])
 

from contextlib import ExitStack

import concourse.mybir as mybir

F32 = mybir.dt.float32
BF16 = mybir.dt.bfloat16
I32 = mybir.dt.int32
U32 = mybir.dt.uint32
U16 = mybir.dt.uint16
U8 = mybir.dt.uint8
FP8X4 = mybir.dt.float8_e4m3fn_x4
ACT = mybir.ActivationFunctionType

P = 128
PACK = 4
QUAD = 32
LIST_ROWS = 16
K, H = 512, 512
T, W = 2048, 1024
S, V = 512, 512
HALF = 256
M_SCALAR = 84
V_ROW = 4
FLOPS = 2 * K * H * S + 2 * K * S * V + 2 * H * S * V


def tile_picked_zwd_sigmoid_p_kernel(tc, x_words, x_scales, e_words, e_scales, v_words, v_scales, gT, w1, offs, cand, out):
    nc = tc.nc
    with ExitStack() as ctx:
        lists = ctx.enter_context(tc.tile_pool(name="lists", bufs=1))
        sb = ctx.enter_context(tc.tile_pool(name="sb", bufs=1))
        psum = ctx.enter_context(tc.psum_pool(name="psum", bufs=1))

        offs_sb = lists.tile([P, S // LIST_ROWS], U16, name="offs_sb")
        cand_sb = lists.tile([P, V // LIST_ROWS], U16, name="cand_sb")

        def tile(shape, dtype, name, reuse=None):
            return sb.tile(shape, dtype, name=name, tag=reuse or name, align_bytes=256)

        def load_words(words, name):
            table = tile([P, words.shape[2]], I32, name)
            nc.sync.dma_start(out=table[:], in_=words[0].rearrange("p n t -> p (n t)").bitcast(I32))
            return table

        def load_scales(table, rows, first_row):
            nc.sync.dma_start(out=table[first_row:P:8, :].bitcast(I32), in_=rows[0].bitcast(I32))

        def place_scales(plane, picked, first_row):
            for r in range(4):
                nc.sync.dma_start(out=plane[first_row + r : P : QUAD, :].bitcast(I32), in_=picked[first_row + 8 * r : P : QUAD, :].bitcast(I32))

        def gather(window, dtype, offsets, n, name, reuse=None):
            picked = tile([P, n], dtype, name, reuse)
            nc.vector.tensor_copy(out=picked[:], in_=window[:].bitcast(dtype).indirect(offsets))
            return picked

        def quantize(src, n, name):
            codes = tile([P, n], U32, name + "_codes")
            plane = tile([P, n], U8, name + "_plane")
            nc.vector.quantize_mx(out=codes[:].bitcast(FP8X4), scales=plane[:], in_=src)
            return codes, plane

        es_tab = tile([P, W], U8, "es_tab")
        vs_tab = tile([P, W], U8, "vs_tab")
        xs_tab = tile([P, T], U8, "xs_tab")
        v_plane = tile([P, V], U8, "v_plane")
        ex_plane = tile([P, V + S], U8, "ex_plane")
        for cleared in (vs_tab, es_tab, xs_tab, v_plane, ex_plane):
            nc.vector.memset(cleared[:].bitcast(I32), 0)

        w_raw = tile([P, PACK, H], F32, "w_raw")
        w_flat = w_raw[:].rearrange("p j c -> p (j c)")
        w_rows = w1.rearrange("(p j) c -> p (j c)", j=PACK)
        nc.scalar.dma_start(out=w_flat[0:P:2, :], in_=w_rows[0:P:2, :])
        nc.sync.dma_start(cand_sb[:], cand)
        nc.sync.dma_start(offs_sb[:], offs)
        load_scales(vs_tab, v_scales, V_ROW)
        load_scales(es_tab, e_scales, 0)
        load_scales(xs_tab, x_scales, 0)
        nc.sync.dma_start(out=w_flat[1:P:2, :], in_=w_rows[1:P:2, :])

        warm_in = tile([P, 1], F32, "warm_in")
        warm_out = tile([P, 1], F32, "warm_out")
        nc.gpsimd.memset(warm_in[:], 0.0)
        nc.scalar.activation(warm_out[:], warm_in[:], ACT.Sigmoid)

        g_raw = tile([P, PACK, S], F32, "g_raw")
        nc.sync.dma_start(out=g_raw[:], in_=gT.rearrange("(p j) c -> p j c", j=PACK))
        e_tab = load_words(e_words, "e_tab")

        v_picked = gather(vs_tab, U8, cand_sb[:], V, "v_picked")
        v_tab = load_words(v_words, "v_tab")
        place_scales(v_plane, v_picked, V_ROW)
        x_tab = load_words(x_words, "x_tab")
        ex_picked = tile([P, V + S], U8, "ex_picked")
        nc.vector.tensor_copy(out=ex_picked[:, 0:V], in_=es_tab[:].indirect(cand_sb[:]))
        nc.vector.tensor_copy(out=ex_picked[:, V : V + S], in_=xs_tab[:].indirect(offs_sb[:]))
        place_scales(ex_plane, ex_picked, 0)

        w_bf = tile([P, H * PACK], BF16, "w_bf")
        w_out = w_bf[:].rearrange("p (t m j) -> p m j t", t=PACK, j=PACK)
        w_in = w_raw[:].rearrange("p j (m t) -> p m j t", t=PACK)
        nc.scalar.copy(out=w_out[:, 0:M_SCALAR], in_=w_in[:, 0:M_SCALAR])
        nc.gpsimd.tensor_scalar(
            w_bf[:].rearrange("p (t m j) -> p m t j", t=PACK, j=PACK)[:, M_SCALAR:P],
            w_raw[:].rearrange("p j (m t) -> p m t j", t=PACK)[:, M_SCALAR:P],
            1.0,
            0.0,
            mybir.AluOpType.mult,
            mybir.AluOpType.add,
        )
        w_codes, w_plane = quantize(w_bf[:], H, "w")

        g_bf = tile([P, S * PACK], BF16, "g_bf")
        g_codes = tile([P, S], U32, "g_codes")
        g_plane = tile([P, S], U8, "g_plane")
        shares = [(nc.scalar.copy, 0, P), (nc.vector.tensor_copy, P, 3 * P // 2), (nc.scalar.copy, 3 * P // 2, HALF), (nc.scalar.copy, HALF, HALF + P), (nc.scalar.copy, HALF + P, S)]
        for cast, u0, u1 in shares:
            cast(
                out=g_bf[:, PACK * u0 : PACK * u1].rearrange("p (c i j) -> p c j i", i=4, j=PACK),
                in_=g_raw[:, :, u0:u1].rearrange("p j (c i) -> p c j i", i=4),
            )
        for u0, u1 in ((0, P), (P, HALF), (HALF, S)):
            nc.vector.quantize_mx(out=g_codes[:, u0:u1].bitcast(FP8X4), scales=g_plane[:, u0:u1], in_=g_bf[:, PACK * u0 : PACK * u1])
        e_codes = gather(e_tab, U32, cand_sb[:], V, "e_codes")
        v_codes = gather(v_tab, U32, cand_sb[:], V, "v_codes")

        def mx_pass(acc, stationary, moving, start, stop):
            nc.tensor.matmul_mx(
                out=acc,
                lhsT=stationary[0].bitcast(FP8X4),
                lhsT_scale=stationary[1],
                rhs=moving[0].bitcast(FP8X4),
                rhs_scale=moving[1],
                start=start,
                stop=stop,
            )

        warm_ps = psum.tile([P, H], F32, name="warm_ps", tag="y_ps3")
        mx_pass(warm_ps[:], (w_codes[:, 0:P], w_plane[:, 0:P]), (w_codes[:], w_plane[:]), True, True)

        def hidden(c, h_bf):
            users = slice(P * c, P * (c + 1))
            h_ps = psum.tile([P, PACK, P], F32, name=f"h_ps{c}", tag=f"h_ps{c}")
            for t in range(PACK):
                channels = slice(P * t, P * (t + 1))
                mx_pass(h_ps[:, t, :], (w_codes[:, channels], w_plane[:, channels]), (g_codes[:, users], g_plane[:, users]), True, True)
            nc.scalar.activation(h_bf.rearrange("p (n t) -> p n t", t=PACK), h_ps[:].rearrange("p t n -> p n t"), ACT.Relu)

        def quantize_hidden(sources, name, reuse=None):
            codes = tile([P, HALF], U32, name + "_codes", reuse)
            plane = tile([P, HALF], U8, name + "_plane")
            width = HALF // len(sources)
            for k, source in enumerate(sources):
                users = slice(width * k, width * (k + 1))
                nc.vector.quantize_mx(out=codes[:, users].bitcast(FP8X4), scales=plane[:, users], in_=source[:])
            return [(codes[:, u : u + P], plane[:, u : u + P]) for u in (0, P)]

        def gather_part(table, offsets, first, n, name, reuse=None):
            return gather(table, U32, offsets[:, first // LIST_ROWS : (first + n) // LIST_ROWS], n, name, reuse)

        h_early = [tile([P, P * PACK], BF16, f"h_bf{c}") for c in (0, 1)]
        for c in (0, 1):
            hidden(c, h_early[c][:])
        h_q = quantize_hidden(h_early, "h_early")
        h_late = [tile([P, P * PACK], BF16, f"h_bf{c}") for c in (2, 3)]
        for c in (2, 3):
            hidden(c, h_late[c - 2][:])
        x_codes = [gather_part(x_tab, offs_sb, P * c, P, f"x_codes{c}") for c in range(3)]
        h_q.extend(quantize_hidden(h_late, "h_late", "ex_picked"))
        x_codes.append(gather_part(x_tab, offs_sb, P * 3, P, "x_codes3", "h_bf2"))

        pieces = [(0, 0, HALF), (0, HALF, V)] + [(c, 0, V) for c in range(1, S // P)]
        for c, n0, n1 in pieces:
            y_ps = psum.tile([P, n1 - n0], F32, name=f"y_ps{c}_{n0}", tag="h_ps0" if n0 > 0 else f"y_ps{c}")
            deep = (h_q[c], (v_codes[:, n0:n1], v_plane[V_ROW:P, n0:n1]))
            wide = ((x_codes[c][:], ex_plane[:, V + P * c : V + P * (c + 1)]), (e_codes[:, n0:n1], ex_plane[:, n0:n1]))
            first, second = (wide, deep) if c == 2 else (deep, wide)
            mx_pass(y_ps[:], first[0], first[1], True, False)
            mx_pass(y_ps[:], second[0], second[1], False, True)
            scores = tile([P, n1 - n0], F32, f"scores{c}_{n0}")
            nc.scalar.activation(scores[:], y_ps[:], ACT.Sigmoid)
            nc.sync.dma_start(out=out[P * c : P * (c + 1), n0:n1], in_=scores[:])
